import numpy as np
import ml_dtypes


def mxq(x, axis, fmt="e4m3"):
    dtype, down = {"e4m3": (ml_dtypes.float8_e4m3fn, 7), "e5m2": (ml_dtypes.float8_e5m2, 14)}[fmt]
    v = np.moveaxis(np.asarray(x, np.float32).astype(ml_dtypes.bfloat16).astype(np.float64), axis, -1)
    blocks = v.reshape(v.shape[:-1] + (-1, 32))
    amax = np.abs(blocks).max(-1, keepdims=True)
    byte = np.maximum(np.where(amax > 0, np.frexp(amax)[1] - 1 + 127, 0) - down, 1)
    scale = np.exp2(byte - 127.0)
    codes = (blocks / scale).astype(np.float32).astype(dtype).astype(np.float64)
    return np.moveaxis((codes * scale).reshape(v.shape), -1, axis)


WIDE = False


def mx_kscale(k):
    if not WIDE:
        return np.ones(k)
    levels = np.array([10, -10, 5, -5, 0])
    if k % 512:
        return np.exp2(np.random.permutation(np.resize(levels, k // 32))).repeat(32)
    a = np.empty((k // 512, 16))
    for p in range(k // 512):
        a[p, :8] = np.random.permutation(np.resize(levels, 8))
        for g in range(8):
            far = levels[np.abs(levels - a[p, g]) >= 10]
            a[p, g + 8] = far[np.random.randint(len(far))]
    return np.exp2(a.ravel()).repeat(32)


def f64(x):
    return np.asarray(x).astype(np.float64)


def striped8(idx):
    return np.concatenate([x.reshape(-1, 16).T for x in idx]).astype(np.uint16)


def runs(offs, k):
    lists = np.stack([offs[16 * r : 16 * r + 16].T.reshape(-1) for r in range(8)]).astype(np.int64)
    return lists[np.arange(k) % 512 // 64]


def pack_weight(w):
    k, n = w.shape
    w = f64(np.asarray(w, np.float32).astype(ml_dtypes.bfloat16)).reshape(k // 32, 32, n)
    amax = np.abs(w).max(1)
    byte = np.clip(np.where(amax > 0, np.frexp(amax)[1] - 1 + 127 - 7, 1), 1, 254)
    scaled = (w * np.exp2(127.0 - byte)[:, None, :]).reshape(k, n).astype(np.float32)
    words = np.ascontiguousarray(scaled.reshape(k // 512, 128, 4, n).transpose(0, 1, 3, 2)).astype(ml_dtypes.float8_e4m3fn).view(np.uint8)
    return words, np.ascontiguousarray(byte.astype(np.uint8).reshape(k // 512, 16, n))


def unpack_weight(words, scales):
    g, p, n, _ = words.shape
    vals = np.ascontiguousarray(words).view(ml_dtypes.float8_e4m3fn).astype(np.float64) * np.repeat(np.exp2(scales.astype(np.float64) - 127.0), 8, axis=1)[..., None]
    return vals.transpose(0, 1, 3, 2).reshape(g * 512, n)


def gelu(v):
    return 0.5 * v * (1.0 + np.tanh(np.sqrt(2.0 / np.pi) * (v + 0.044715 * v**3)))

def planes(y):
    n, m = y.shape
    v = y.astype(np.float32).astype(ml_dtypes.bfloat16).astype(np.float64).reshape(n // 32, 32, m)
    top = np.abs(v).max(1)
    byte = np.clip(np.where(top > 0, np.frexp(top)[1] - 1 + 127 - 7, 1), 1, 254)
    codes = (v * np.exp2(127.0 - byte)[:, None, :]).reshape(n, m).astype(np.float32).astype(ml_dtypes.float8_e4m3fn).view(np.uint8)
    words = codes.reshape(n // 512, 128, 4, m).transpose(0, 1, 3, 2)
    return np.ascontiguousarray(words), np.ascontiguousarray(byte.astype(np.uint8).reshape(n // 512, 16, m))


K, T, S, H = 512, 2048, 1024, 512


def setup_inputs():
    n = np.random.standard_normal
    s = mx_kscale(K)[:, None]
    u = mx_kscale(H)
    packed_xT = pack_weight(n((K, T)) * s)
    packed_w2 = pack_weight(n((H, H)) / np.sqrt(H) / u[:, None])
    return {
        "x_words": packed_xT[0],
        "x_scales": packed_xT[1],
        "w1": (n((K, H)) / np.sqrt(K) / s * u).astype(np.float32),
        "w2_words": packed_w2[0],
        "w2_scales": packed_w2[1],
        "pos": (0.5 * n((H, S)) * u[:, None]).astype(np.float32),
        "offs": striped8(np.random.randint(0, T, (8, S))),
    }


def reference(x_words, x_scales, w1, w2_words, w2_scales, pos, offs):
    xq = unpack_weight(x_words, x_scales)[np.arange(K)[:, None], runs(offs, K)]
    h = gelu((mxq(f64(w1), 0, "e4m3").T @ xq) + f64(pos))
    out_0 = unpack_weight(w2_words, w2_scales).T @ mxq(h, 0, "e4m3")
    return (out_0,) + planes(out_0)

@@ -1,0 +1,219 @@
+from contextlib import ExitStack
+
+import concourse.mybir as mybir
+
+K, T, S, H = 512, 2048, 1024, 512
+FLOPS = 2 * K * H * S + 2 * H * H * S
+
+F32 = mybir.dt.float32
+BF16 = mybir.dt.bfloat16
+I32 = mybir.dt.int32
+U32 = mybir.dt.uint32
+U16 = mybir.dt.uint16
+U8 = mybir.dt.uint8
+FP8X4 = mybir.dt.float8_e4m3fn_x4
+GELU = mybir.ActivationFunctionType.Gelu_apprx_tanh
+ADD = mybir.AluOpType.add
+
+P = 128
+PACK = 4
+GATHER = 256
+CHUNKS = ((0, 128), (128, 384), (384, 640), (640, 896), (896, 1024))
+N_CHUNKS = len(CHUNKS)
+W1_VECTOR_M = 40
+BANK = 512
+W1_PIECES = 2
+POS_PIECES = ((0, 128), (128, 384), (384, 640), (640, 1024))
+
+
+def tile_picked_phpq_gelu_po_kernel(
+    tc, x_words, x_scales, w1, w2_words, w2_scales, pos, offs, out_0, out_1, out_2
+):
+    nc = tc.nc
+    with ExitStack() as ctx:
+        keep = ctx.enter_context(tc.tile_pool(name="keep", bufs=1))
+        psum = ctx.enter_context(tc.psum_pool(name="psum", bufs=4))
+
+        offsets = keep.tile([P, S // 16], U16, name="offsets")
+        nc.sync.dma_start(offsets[:], offs)
+
+        xs_win = keep.tile([P, T], U8, name="xs_win", tag="slot_a")
+        nc.sync.dma_start(
+            xs_win[:].bitcast(I32), x_scales[0].bitcast(I32).unsqueeze(1).to_broadcast([16, 8, T // 4])
+        )
+        w2s_raw = keep.tile([P, H], U8, name="w2s_raw")
+        for q in range(4):
+            nc.scalar.dma_start(
+                w2s_raw[32 * q : 32 * q + 32, :].bitcast(I32),
+                w2_scales[0, 4 * q : 4 * q + 4, :].bitcast(I32).unsqueeze(0).to_broadcast([8, 4, H // 4]),
+            )
+        warm = keep.tile([P, 1], F32, name="warm")
+        nc.vector.memset(warm[:], 0.0)
+        warm_out = keep.tile([P, 1], F32, name="warm_out")
+        nc.scalar.activation(warm_out[:], warm[:], GELU)
+
+        xw_win = keep.tile([P, T], U32, name="xw_win")
+        nc.sync.dma_start(xw_win[:].bitcast(I32), x_words[0].rearrange("p n t -> p (n t)").bitcast(I32))
+
+        w1_rows = w1.rearrange("(p j) c -> p j c", j=PACK)
+        piece = H // W1_PIECES
+        w1_raw = []
+        for a in range(W1_PIECES):
+            raw = keep.tile([P, PACK, piece], F32, name=f"w1_raw{a}", tag=f"slot_w{a}")
+            nc.sync.dma_start(raw[:], w1_rows[:, :, a * piece : (a + 1) * piece])
+            w1_raw.append(raw)
+
+        xs_plane = keep.tile([P, S], U8, name="xs_plane", align_bytes=64)
+        nc.vector.memset(xs_plane[:].bitcast(I32), 0)
+
+        pos_rows = pos.rearrange("(p t) s -> p t s", t=PACK)
+        pos_tiles = []
+
+        def load_pos(i, tag, eng=nc.sync):
+            a, b = POS_PIECES[i]
+            tile = keep.tile([P, PACK, b - a], F32, name=f"pos{i}", tag=tag)
+            eng.dma_start(tile[:], pos_rows[:, :, a:b])
+            pos_tiles.append(tile)
+
+
+        load_pos(0, "pos0")
+        xs_got = keep.tile([P, S], U8, name="xs_got", tag="slot_b")
+        nc.vector.tensor_copy(xs_got[:], xs_win[:].indirect(offsets[:]))
+        for q in range(4):
+            nc.scalar.dma_start(xs_plane[32 * q : 32 * q + 4, :].bitcast(I32), xs_got[32 * q : 32 * q + 32 : 8, :].bitcast(I32))
+        load_pos(1, "slot_a", nc.scalar)
+        w2w_raw = keep.tile([P, H], I32, name="w2w_raw", tag="slot_b")
+        nc.sync.dma_start(w2w_raw[:], w2_words[0].rearrange("p n t -> p (n t)").bitcast(I32))
+
+        def pos_cols(c):
+            for (a, b), tile in zip(POS_PIECES, pos_tiles):
+                if a <= CHUNKS[c][0] < b:
+                    return tile[:, :, CHUNKS[c][0] - a : CHUNKS[c][1] - a]
+
+        EARLY = 640
+        xq_early = keep.tile([P, EARLY], U32, name="xq_early", align_bytes=64)
+        nc.vector.tensor_copy(xq_early[:], xw_win[:].indirect(offsets[:, 0 : EARLY // 16]))
+
+        w1_bf = keep.tile([P, PACK, P, PACK], BF16, name="w1_bf", align_bytes=64, tag="slot_e")
+        ms = piece // PACK
+
+        def round_w1(copy, a, m0, m1):
+            copy(
+                w1_bf[:, :, a * ms + m0 : a * ms + m1, :].rearrange("p t m j -> p m t j"),
+                w1_raw[a][:, :, PACK * m0 : PACK * m1].rearrange("p j (m t) -> p m t j", t=PACK),
+            )
+
+        round_w1(nc.scalar.copy, 0, 0, ms)
+        round_w1(nc.vector.tensor_copy, 1, 0, W1_VECTOR_M)
+        round_w1(nc.scalar.copy, 1, W1_VECTOR_M, ms)
+        load_pos(2, "slot_w0")
+        load_pos(3, "slot_w1")
+        w1_q = keep.tile([P, H], U32, name="w1_q", align_bytes=64)
+        w1_s = keep.tile([P, H], U8, name="w1_s", align_bytes=64)
+        for t in range(PACK):
+            cols = slice(t * P, (t + 1) * P)
+            nc.vector.quantize_mx(
+                out=w1_q[:, cols].bitcast(FP8X4),
+                scales=w1_s[:, cols],
+                in_=w1_bf[:, t, :, :].rearrange("p m j -> p (m j)"),
+            )
+        xq_late = keep.tile([P, S - EARLY], U32, name="xq_late", align_bytes=64, tag="slot_e")
+        nc.vector.tensor_copy(xq_late[:], xw_win[:].indirect(offsets[:, EARLY // 16 : S // 16]))
+
+        def x_codes(c):
+            a, b = CHUNKS[c]
+            return xq_early[:, a:b] if b <= EARLY else xq_late[:, a - EARLY : b - EARLY]
+
+        w2_q = keep.tile([P, H], I32, name="w2_q", align_bytes=64)
+        w2_s = keep.tile([P, H], U8, name="w2_s", align_bytes=64)
+
+        def deal_w2():
+            nc.vector.tensor_copy(
+                w2_q[:].rearrange("p (t b i) -> p b t i", t=PACK, i=4),
+                w2w_raw[:].rearrange("p (b i t) -> p b t i", t=PACK, i=4),
+            )
+            nc.vector.tensor_copy(
+                w2_s[:].rearrange("p (t m) -> p m t", t=PACK), w2s_raw[:].rearrange("p (m t) -> p m t", t=PACK)
+            )
+
+        out_q = keep.tile([P, S], U32, name="out_q", align_bytes=64)
+        out_s = keep.tile([P, S], U8, name="out_s", align_bytes=64)
+        out_rows = out_0.rearrange("(p t) s -> p t s", t=PACK)
+        out_words = out_1[0].rearrange("p n t -> p (n t)").bitcast(I32)
+
+        def product(name, n, w_q, w_s, codes, scales):
+            banks = []
+            per_bank = BANK // n
+            for b in range(PACK // per_bank):
+                bank = psum.tile([P, per_bank, n], F32, name=name)
+                for u in range(per_bank):
+                    cols = slice((b * per_bank + u) * P, (b * per_bank + u + 1) * P)
+                    nc.tensor.matmul_mx(
+                        out=bank[:, u, :],
+                        lhsT=w_q[:, cols].bitcast(FP8X4),
+                        lhsT_scale=w_s[:, cols],
+                        rhs=codes.bitcast(FP8X4),
+                        rhs_scale=scales,
+                        start=True,
+                        stop=True,
+                    )
+                banks.append((slice(b * per_bank, (b + 1) * per_bank), bank))
+            return banks
+
+        pre = {}
+        h_bf = {}
+        y = {}
+
+        def layer1(c):
+            cols = slice(*CHUNKS[c])
+            n = cols.stop - cols.start
+            banks = product("acc1", n, w1_q, w1_s, x_codes(c), xs_plane[:, cols])
+            pre[c] = keep.tile([P, PACK, n], F32, name=f"pre{c}")
+            for ts, bank in banks:
+                nc.vector.tensor_tensor(pre[c][:, ts, :], bank[:], pos_cols(c)[:, ts, :], ADD)
+            h_bf[c] = keep.tile([P, n, PACK], BF16, name=f"h_bf{c}", align_bytes=64)
+            nc.scalar.activation(
+                h_bf[c][:].rearrange("p (g i) t -> p g t i", i=4),
+                pre[c][:].rearrange("p t (g i) -> p g t i", i=4),
+                GELU,
+            )
+
+        def layer2(c):
+            cols = slice(*CHUNKS[c])
+            n = cols.stop - cols.start
+            h_q = keep.tile([P, n], U32, name=f"h_q{c}", align_bytes=64)
+            h_s = keep.tile([P, n], U8, name=f"h_s{c}", align_bytes=64)
+            nc.vector.quantize_mx(
+                out=h_q[:].bitcast(FP8X4), scales=h_s[:], in_=h_bf[c][:].rearrange("p n t -> p (n t)")
+            )
+            banks = product("acc2", n, w2_q, w2_s, h_q[:], h_s[:])
+            y[c] = keep.tile([P, PACK, n], F32, name=f"y{c}")
+            for ts, bank in banks:
+                nc.scalar.copy(y[c][:, ts, :], bank[:])
+            nc.sync.dma_start(out_rows[:, :, cols], y[c][:])
+
+        def planes(c):
+            cols = slice(*CHUNKS[c])
+            n = cols.stop - cols.start
+            y_bf = keep.tile([P, n, PACK], BF16, name=f"y_bf{c}", align_bytes=64)
+            nc.vector.tensor_copy(
+                y_bf[:].rearrange("p (g i) t -> p g t i", i=4), y[c][:].rearrange("p t (g i) -> p g t i", i=4)
+            )
+            nc.vector.quantize_mx(
+                out=out_q[:, cols].bitcast(FP8X4), scales=out_s[:, cols], in_=y_bf[:].rearrange("p n t -> p (n t)")
+            )
+            nc.sync.dma_start(out_words[:, cols], out_q[:, cols].bitcast(I32))
+
+        for step in range(N_CHUNKS + 2):
+            if step < N_CHUNKS:
+                layer1(step)
+            if step == 0:
+                deal_w2()
+            if 0 <= step - 1 < N_CHUNKS:
+                layer2(step - 1)
+            if 0 <= step - 2 < N_CHUNKS:
+                planes(step - 2)
+
+        for q in range(4):
+            eng = nc.sync if q % 2 == 0 else nc.scalar
+            eng.dma_start(out_2[0, 4 * q : 4 * q + 4, :].bitcast(I32), out_s[32 * q : 32 * q + 4, :].bitcast(I32))

@@ -17,13 +17,17 @@ ADD = mybir.AluOpType.add
 
 P = 128
 PACK = 4
-GATHER = 256
-CHUNKS = ((0, 128), (128, 384), (384, 640), (640, 896), (896, 1024))
-N_CHUNKS = len(CHUNKS)
+UNIT = 128
+N_UNITS = S // UNIT
+EARLY = 768
+PLANE_GROUPS = ((0, 2), (2, 4), (4, 6), (6, 7), (7, 8))
+OUT_GROUPS = ((0, 2), (2, 4), (4, 6), (6, 7), (7, 8))
+WORD_GROUPS = ((0, 4), (4, 7), (7, 8))
+COPY_LAG = 3
+VECTOR_COPIES = (4,)
 W1_VECTOR_M = 40
-BANK = 512
 W1_PIECES = 2
-POS_PIECES = ((0, 128), (128, 384), (384, 640), (640, 1024))
+POS_PIECES = ((0, 256), (256, 512), (512, 768), (768, 1024))
 
 
 def tile_picked_phpq_gelu_po_kernel(
@@ -32,12 +36,13 @@ def tile_picked_phpq_gelu_po_kernel(
     nc = tc.nc
     with ExitStack() as ctx:
         keep = ctx.enter_context(tc.tile_pool(name="keep", bufs=1))
+        shared = ctx.enter_context(tc.tile_pool(name="shared", bufs=1))
         psum = ctx.enter_context(tc.psum_pool(name="psum", bufs=4))
 
         offsets = keep.tile([P, S // 16], U16, name="offsets")
         nc.sync.dma_start(offsets[:], offs)
 
-        xs_win = keep.tile([P, T], U8, name="xs_win", tag="slot_a")
+        xs_win = shared.tile([P, T], U8, name="xs_win", offset=15360)
         nc.sync.dma_start(
             xs_win[:].bitcast(I32), x_scales[0].bitcast(I32).unsqueeze(1).to_broadcast([16, 8, T // 4])
         )
@@ -59,7 +64,7 @@ def tile_picked_phpq_gelu_po_kernel(
         piece = H // W1_PIECES
         w1_raw = []
         for a in range(W1_PIECES):
-            raw = keep.tile([P, PACK, piece], F32, name=f"w1_raw{a}", tag=f"slot_w{a}")
+            raw = keep.tile([P, PACK, piece], F32, name=f"w1_raw{a}")
             nc.sync.dma_start(raw[:], w1_rows[:, :, a * piece : (a + 1) * piece])
             w1_raw.append(raw)
 
@@ -67,34 +72,27 @@ def tile_picked_phpq_gelu_po_kernel(
         nc.vector.memset(xs_plane[:].bitcast(I32), 0)
 
         pos_rows = pos.rearrange("(p t) s -> p t s", t=PACK)
-        pos_tiles = []
+        pos_sb = shared.tile([P, PACK, S], F32, name="pos_sb", offset=0)
 
-        def load_pos(i, tag, eng=nc.sync):
+        def load_pos(i):
             a, b = POS_PIECES[i]
-            tile = keep.tile([P, PACK, b - a], F32, name=f"pos{i}", tag=tag)
-            eng.dma_start(tile[:], pos_rows[:, :, a:b])
-            pos_tiles.append(tile)
+            nc.sync.dma_start(pos_sb[:, :, a:b], pos_rows[:, :, a:b])
 
-
-        load_pos(0, "pos0")
-        xs_got = keep.tile([P, S], U8, name="xs_got", tag="slot_b")
+        xs_got = keep.tile([P, S], U8, name="xs_got")
         nc.vector.tensor_copy(xs_got[:], xs_win[:].indirect(offsets[:]))
         for q in range(4):
-            nc.scalar.dma_start(xs_plane[32 * q : 32 * q + 4, :].bitcast(I32), xs_got[32 * q : 32 * q + 32 : 8, :].bitcast(I32))
-        load_pos(1, "slot_a", nc.scalar)
-        w2w_raw = keep.tile([P, H], I32, name="w2w_raw", tag="slot_b")
+            nc.sync.dma_start(xs_plane[32 * q : 32 * q + 4, :].bitcast(I32), xs_got[32 * q : 32 * q + 32 : 8, :].bitcast(I32))
+        load_pos(0)
+        w2w_raw = shared.tile([P, H], I32, name="w2w_raw", offset=16384)
         nc.sync.dma_start(w2w_raw[:], w2_words[0].rearrange("p n t -> p (n t)").bitcast(I32))
+        load_pos(1)
+        load_pos(2)
+        load_pos(3)
 
-        def pos_cols(c):
-            for (a, b), tile in zip(POS_PIECES, pos_tiles):
-                if a <= CHUNKS[c][0] < b:
-                    return tile[:, :, CHUNKS[c][0] - a : CHUNKS[c][1] - a]
-
-        EARLY = 640
         xq_early = keep.tile([P, EARLY], U32, name="xq_early", align_bytes=64)
         nc.vector.tensor_copy(xq_early[:], xw_win[:].indirect(offsets[:, 0 : EARLY // 16]))
 
-        w1_bf = keep.tile([P, PACK, P, PACK], BF16, name="w1_bf", align_bytes=64, tag="slot_e")
+        w1_bf = shared.tile([P, PACK, P, PACK], BF16, name="w1_bf", align_bytes=64, offset=18432)
         ms = piece // PACK
 
         def round_w1(copy, a, m0, m1):
@@ -106,8 +104,6 @@ def tile_picked_phpq_gelu_po_kernel(
         round_w1(nc.scalar.copy, 0, 0, ms)
         round_w1(nc.vector.tensor_copy, 1, 0, W1_VECTOR_M)
         round_w1(nc.scalar.copy, 1, W1_VECTOR_M, ms)
-        load_pos(2, "slot_w0")
-        load_pos(3, "slot_w1")
         w1_q = keep.tile([P, H], U32, name="w1_q", align_bytes=64)
         w1_s = keep.tile([P, H], U8, name="w1_s", align_bytes=64)
         for t in range(PACK):
@@ -117,23 +113,20 @@ def tile_picked_phpq_gelu_po_kernel(
                 scales=w1_s[:, cols],
                 in_=w1_bf[:, t, :, :].rearrange("p m j -> p (m j)"),
             )
-        xq_late = keep.tile([P, S - EARLY], U32, name="xq_late", align_bytes=64, tag="slot_e")
+
+        xq_late = shared.tile([P, S - EARLY], U32, name="xq_late", align_bytes=64, offset=20992)
         nc.vector.tensor_copy(xq_late[:], xw_win[:].indirect(offsets[:, EARLY // 16 : S // 16]))
 
-        def x_codes(c):
-            a, b = CHUNKS[c]
-            return xq_early[:, a:b] if b <= EARLY else xq_late[:, a - EARLY : b - EARLY]
-
-        w2_q = keep.tile([P, H], I32, name="w2_q", align_bytes=64)
-        w2_s = keep.tile([P, H], U8, name="w2_s", align_bytes=64)
+        w2_q = shared.tile([P, H], I32, name="w2_q", align_bytes=64, offset=18432)
+        w2_s = shared.tile([P, H], U8, name="w2_s", align_bytes=64, offset=20480)
 
         def deal_w2():
             nc.vector.tensor_copy(
-                w2_q[:].rearrange("p (t b i) -> p b t i", t=PACK, i=4),
-                w2w_raw[:].rearrange("p (b i t) -> p b t i", t=PACK, i=4),
+                w2_s[:].rearrange("p (t m) -> p t m", t=PACK), w2s_raw[:].rearrange("p (m t) -> p t m", t=PACK)
             )
             nc.vector.tensor_copy(
-                w2_s[:].rearrange("p (t m) -> p m t", t=PACK), w2s_raw[:].rearrange("p (m t) -> p m t", t=PACK)
+                w2_q[:].rearrange("p (t b i) -> p b t i", t=PACK, i=4),
+                w2w_raw[:].rearrange("p (b i t) -> p b t i", t=PACK, i=4),
             )
 
         out_q = keep.tile([P, S], U32, name="out_q", align_bytes=64)
@@ -141,78 +134,88 @@ def tile_picked_phpq_gelu_po_kernel(
         out_rows = out_0.rearrange("(p t) s -> p t s", t=PACK)
         out_words = out_1[0].rearrange("p n t -> p (n t)").bitcast(I32)
 
-        def product(name, n, w_q, w_s, codes, scales):
-            banks = []
-            per_bank = BANK // n
-            for b in range(PACK // per_bank):
-                bank = psum.tile([P, per_bank, n], F32, name=name)
-                for u in range(per_bank):
-                    cols = slice((b * per_bank + u) * P, (b * per_bank + u + 1) * P)
-                    nc.tensor.matmul_mx(
-                        out=bank[:, u, :],
-                        lhsT=w_q[:, cols].bitcast(FP8X4),
-                        lhsT_scale=w_s[:, cols],
-                        rhs=codes.bitcast(FP8X4),
-                        rhs_scale=scales,
-                        start=True,
-                        stop=True,
-                    )
-                banks.append((slice(b * per_bank, (b + 1) * per_bank), bank))
-            return banks
+        def columns(u0, u1):
+            return slice(u0 * UNIT, u1 * UNIT)
 
-        pre = {}
+        def product(name, w_q, w_s, codes, scales):
+            bank = psum.tile([P, PACK, UNIT], F32, name=name)
+            for t in range(PACK):
+                cols = slice(t * P, (t + 1) * P)
+                nc.tensor.matmul_mx(
+                    out=bank[:, t, :],
+                    lhsT=w_q[:, cols].bitcast(FP8X4),
+                    lhsT_scale=w_s[:, cols],
+                    rhs=codes.bitcast(FP8X4),
+                    rhs_scale=scales,
+                    start=True,
+                    stop=True,
+                )
+            return bank
+
         h_bf = {}
+        acc2 = {}
         y = {}
+        for a, b in OUT_GROUPS:
+            tile = keep.tile([P, PACK, (b - a) * UNIT], F32, name=f"y{a}")
+            for u in range(a, b):
+                y[u] = (tile, a)
 
-        def layer1(c):
-            cols = slice(*CHUNKS[c])
-            n = cols.stop - cols.start
-            banks = product("acc1", n, w1_q, w1_s, x_codes(c), xs_plane[:, cols])
-            pre[c] = keep.tile([P, PACK, n], F32, name=f"pre{c}")
-            for ts, bank in banks:
-                nc.vector.tensor_tensor(pre[c][:, ts, :], bank[:], pos_cols(c)[:, ts, :], ADD)
-            h_bf[c] = keep.tile([P, n, PACK], BF16, name=f"h_bf{c}", align_bytes=64)
+        def layer1(u):
+            cols = columns(u, u + 1)
+            early = EARLY // UNIT
+            codes = xq_early[:, cols] if u < early else xq_late[:, columns(u - early, u - early + 1)]
+            bank = product("acc1", w1_q, w1_s, codes, xs_plane[:, cols])
+            pre = keep.tile([P, PACK, UNIT], F32, name=f"pre{u}")
+            nc.vector.tensor_tensor(pre[:], bank[:], pos_sb[:, :, cols], ADD)
+            h_bf[u] = keep.tile([P, UNIT, PACK], BF16, name=f"h_bf{u}", align_bytes=64)
             nc.scalar.activation(
-                h_bf[c][:].rearrange("p (g i) t -> p g t i", i=4),
-                pre[c][:].rearrange("p t (g i) -> p g t i", i=4),
+                h_bf[u][:].rearrange("p (g i) t -> p g t i", i=4),
+                pre[:].rearrange("p t (g i) -> p g t i", i=4),
                 GELU,
             )
 
-        def layer2(c):
-            cols = slice(*CHUNKS[c])
-            n = cols.stop - cols.start
-            h_q = keep.tile([P, n], U32, name=f"h_q{c}", align_bytes=64)
-            h_s = keep.tile([P, n], U8, name=f"h_s{c}", align_bytes=64)
+        def layer2(u):
+            h_q = keep.tile([P, UNIT], U32, name=f"h_q{u}", align_bytes=64)
+            h_s = keep.tile([P, UNIT], U8, name=f"h_s{u}", align_bytes=64)
             nc.vector.quantize_mx(
-                out=h_q[:].bitcast(FP8X4), scales=h_s[:], in_=h_bf[c][:].rearrange("p n t -> p (n t)")
+                out=h_q[:].bitcast(FP8X4), scales=h_s[:], in_=h_bf[u][:].rearrange("p n t -> p (n t)")
             )
-            banks = product("acc2", n, w2_q, w2_s, h_q[:], h_s[:])
-            y[c] = keep.tile([P, PACK, n], F32, name=f"y{c}")
-            for ts, bank in banks:
-                nc.scalar.copy(y[c][:, ts, :], bank[:])
-            nc.sync.dma_start(out_rows[:, :, cols], y[c][:])
+            acc2[u] = product("acc2", w2_q, w2_s, h_q[:], h_s[:])
 
-        def planes(c):
-            cols = slice(*CHUNKS[c])
-            n = cols.stop - cols.start
-            y_bf = keep.tile([P, n, PACK], BF16, name=f"y_bf{c}", align_bytes=64)
+        def leave(u):
+            tile, a = y[u]
+            copy = nc.vector.tensor_copy if u in VECTOR_COPIES else nc.scalar.copy
+            copy(tile[:, :, columns(u - a, u - a + 1)], acc2[u][:])
+            for g0, g1 in OUT_GROUPS:
+                if g1 == u + 1:
+                    nc.sync.dma_start(out_rows[:, :, columns(g0, g1)], tile[:])
+
+        def planes(a, b):
+            cols = columns(a, b)
+            tile, first = y[a]
+            y_bf = keep.tile([P, (b - a) * UNIT, PACK], BF16, name=f"y_bf{a}", align_bytes=64)
             nc.vector.tensor_copy(
-                y_bf[:].rearrange("p (g i) t -> p g t i", i=4), y[c][:].rearrange("p t (g i) -> p g t i", i=4)
+                y_bf[:].rearrange("p (g i) t -> p g t i", i=4),
+                tile[:, :, columns(a - first, b - first)].rearrange("p t (g i) -> p g t i", i=4),
             )
             nc.vector.quantize_mx(
                 out=out_q[:, cols].bitcast(FP8X4), scales=out_s[:, cols], in_=y_bf[:].rearrange("p n t -> p (n t)")
             )
-            nc.sync.dma_start(out_words[:, cols], out_q[:, cols].bitcast(I32))
+            for g0, g1 in WORD_GROUPS:
+                if g1 == b:
+                    nc.sync.dma_start(out_words[:, columns(g0, g1)], out_q[:, columns(g0, g1)].bitcast(I32))
 
-        for step in range(N_CHUNKS + 2):
-            if step < N_CHUNKS:
+        for step in range(N_UNITS + COPY_LAG):
+            if step < N_UNITS:
                 layer1(step)
             if step == 0:
                 deal_w2()
-            if 0 <= step - 1 < N_CHUNKS:
+            if 0 <= step - 1 < N_UNITS:
                 layer2(step - 1)
-            if 0 <= step - 2 < N_CHUNKS:
-                planes(step - 2)
+            if 0 <= step - COPY_LAG < N_UNITS:
+                leave(step - COPY_LAG)
+        for a, b in PLANE_GROUPS:
+            planes(a, b)
 
         for q in range(4):
             eng = nc.sync if q % 2 == 0 else nc.scalar

@@ -97,8 +97,8 @@ def tile_picked_phpq_gelu_po_kernel(
 
         def round_w1(copy, a, m0, m1):
             copy(
-                w1_bf[:, :, a * ms + m0 : a * ms + m1, :].rearrange("p t m j -> p m t j"),
-                w1_raw[a][:, :, PACK * m0 : PACK * m1].rearrange("p j (m t) -> p m t j", t=PACK),
+                w1_bf[:, :, a * ms + m0 : a * ms + m1, :].rearrange("p (s e) m j -> p m s j e", e=2),
+                w1_raw[a][:, :, PACK * m0 : PACK * m1].rearrange("p j (m s e) -> p m s j e", s=2, e=2),
             )
 
         round_w1(nc.scalar.copy, 0, 0, ms)
@@ -169,8 +169,8 @@ def tile_picked_phpq_gelu_po_kernel(
             nc.vector.tensor_tensor(pre[:], bank[:], pos_sb[:, :, cols], ADD)
             h_bf[u] = keep.tile([P, UNIT, PACK], BF16, name=f"h_bf{u}", align_bytes=64)
             nc.scalar.activation(
-                h_bf[u][:].rearrange("p (g i) t -> p g t i", i=4),
-                pre[:].rearrange("p t (g i) -> p g t i", i=4),
+                h_bf[u][:].rearrange("p (g i) t -> p g t i", i=2),
+                pre[:].rearrange("p t (g i) -> p g t i", i=2),
                 GELU,
             )
 
@@ -195,8 +195,8 @@ def tile_picked_phpq_gelu_po_kernel(
             tile, first = y[a]
             y_bf = keep.tile([P, (b - a) * UNIT, PACK], BF16, name=f"y_bf{a}", align_bytes=64)
             nc.vector.tensor_copy(
-                y_bf[:].rearrange("p (g i) t -> p g t i", i=4),
-                tile[:, :, columns(a - first, b - first)].rearrange("p t (g i) -> p g t i", i=4),
+                y_bf[:].rearrange("p (g i) t -> p g t i", i=2),
+                tile[:, :, columns(a - first, b - first)].rearrange("p t (g i) -> p g t i", i=2),
             )
             nc.vector.quantize_mx(
                 out=out_q[:, cols].bitcast(FP8X4), scales=out_s[:, cols], in_=y_bf[:].rearrange("p n t -> p (n t)")

@@ -21,10 +21,10 @@ UNIT = 128
 N_UNITS = S // UNIT
 EARLY = 768
 PLANE_GROUPS = ((0, 2), (2, 4), (4, 6), (6, 7), (7, 8))
-OUT_GROUPS = ((0, 2), (2, 4), (4, 6), (6, 7), (7, 8))
-WORD_GROUPS = ((0, 4), (4, 7), (7, 8))
-COPY_LAG = 3
-VECTOR_COPIES = (4,)
+OUT_GROUPS = ((0, 2), (2, 4), (4, 6), (6, 8))
+WORD_GROUPS = ((0, 2), (2, 4), (4, 8))
+COPY_LAG = 2
+VECTOR_COPIES = (1,)
 W1_VECTOR_M = 40
 W1_PIECES = 2
 POS_PIECES = ((0, 256), (256, 512), (512, 768), (768, 1024))

@@ -20,13 +20,13 @@ PACK = 4
 UNIT = 128
 N_UNITS = S // UNIT
 EARLY = 768
-PLANE_GROUPS = ((0, 2), (2, 4), (4, 6), (6, 7), (7, 8))
+PLANE_GROUPS = tuple((u, u + 1) for u in range(N_UNITS))
 OUT_GROUPS = ((0, 2), (2, 4), (4, 6), (6, 8))
-WORD_GROUPS = ((0, 2), (2, 4), (4, 8))
-COPY_LAG = 2
+WORD_GROUPS = ((0, 2), (2, 6), (6, 8))
+COPY_LAG = 3
 VECTOR_COPIES = (1,)
-W1_VECTOR_M = 40
-W1_PIECES = 2
+W1_VECTOR_M = 80
+W1_PIECES = 1
 POS_PIECES = ((0, 256), (256, 512), (512, 768), (768, 1024))
 
 
@@ -68,6 +68,9 @@ def tile_picked_phpq_gelu_po_kernel(
             nc.sync.dma_start(raw[:], w1_rows[:, :, a * piece : (a + 1) * piece])
             w1_raw.append(raw)
 
+        w2w_raw = keep.tile([P, H], I32, name="w2w_raw")
+        nc.sync.dma_start(w2w_raw[:], w2_words[0].rearrange("p n t -> p (n t)").bitcast(I32))
+
         xs_plane = keep.tile([P, S], U8, name="xs_plane", align_bytes=64)
         nc.vector.memset(xs_plane[:].bitcast(I32), 0)
 
@@ -83,8 +86,6 @@ def tile_picked_phpq_gelu_po_kernel(
         for q in range(4):
             nc.sync.dma_start(xs_plane[32 * q : 32 * q + 4, :].bitcast(I32), xs_got[32 * q : 32 * q + 32 : 8, :].bitcast(I32))
         load_pos(0)
-        w2w_raw = shared.tile([P, H], I32, name="w2w_raw", offset=16384)
-        nc.sync.dma_start(w2w_raw[:], w2_words[0].rearrange("p n t -> p (n t)").bitcast(I32))
         load_pos(1)
         load_pos(2)
         load_pos(3)
@@ -101,9 +102,8 @@ def tile_picked_phpq_gelu_po_kernel(
                 w1_raw[a][:, :, PACK * m0 : PACK * m1].rearrange("p j (m s e) -> p m s j e", s=2, e=2),
             )
 
-        round_w1(nc.scalar.copy, 0, 0, ms)
-        round_w1(nc.vector.tensor_copy, 1, 0, W1_VECTOR_M)
-        round_w1(nc.scalar.copy, 1, W1_VECTOR_M, ms)
+        round_w1(nc.vector.tensor_copy, 0, 0, W1_VECTOR_M)
+        round_w1(nc.scalar.copy, 0, W1_VECTOR_M, ms)
         w1_q = keep.tile([P, H], U32, name="w1_q", align_bytes=64)
         w1_s = keep.tile([P, H], U8, name="w1_s", align_bytes=64)
         for t in range(PACK):

@@ -42,16 +42,16 @@ def tile_picked_phpq_gelu_po_kernel(
         offsets = keep.tile([P, S // 16], U16, name="offsets")
         nc.sync.dma_start(offsets[:], offs)
 
-        xs_win = shared.tile([P, T], U8, name="xs_win", offset=15360)
-        nc.sync.dma_start(
-            xs_win[:].bitcast(I32), x_scales[0].bitcast(I32).unsqueeze(1).to_broadcast([16, 8, T // 4])
-        )
+        xs_win = shared.tile([P, T], U8, name="xs_win", offset=15872)
+        nc.vector.memset(xs_win[:, 0 : T // 2].bitcast(I32), 0)
+        nc.gpsimd.memset(xs_win[:, T // 2 : T].bitcast(I32), 0)
         w2s_raw = keep.tile([P, H], U8, name="w2s_raw")
         for q in range(4):
-            nc.scalar.dma_start(
+            nc.sync.dma_start(
                 w2s_raw[32 * q : 32 * q + 32, :].bitcast(I32),
                 w2_scales[0, 4 * q : 4 * q + 4, :].bitcast(I32).unsqueeze(0).to_broadcast([8, 4, H // 4]),
             )
+        nc.sync.dma_start(xs_win[0:P:8, :].bitcast(I32), x_scales[0].bitcast(I32))
         warm = keep.tile([P, 1], F32, name="warm")
         nc.vector.memset(warm[:], 0.0)
         warm_out = keep.tile([P, 1], F32, name="warm_out")

@@ -20,14 +20,13 @@ PACK = 4
 UNIT = 128
 N_UNITS = S // UNIT
 EARLY = 768
-PLANE_GROUPS = tuple((u, u + 1) for u in range(N_UNITS))
-OUT_GROUPS = ((0, 2), (2, 4), (4, 6), (6, 8))
-WORD_GROUPS = ((0, 2), (2, 6), (6, 8))
-COPY_LAG = 3
+OUT_GROUPS = ((0, 1), (1, 3), (3, 5), (5, 6), (6, 8))
+WORD_GROUPS = ((0, 2), (2, 4), (4, 6), (6, 8))
+COPY_LAG = 2
 VECTOR_COPIES = (1,)
 W1_VECTOR_M = 80
 W1_PIECES = 1
-POS_PIECES = ((0, 256), (256, 512), (512, 768), (768, 1024))
+POS_PIECES = ((128, 384), (384, 640), (640, 896), (896, 1024))
 
 
 def tile_picked_phpq_gelu_po_kernel(
@@ -45,9 +44,12 @@ def tile_picked_phpq_gelu_po_kernel(
         xs_win = shared.tile([P, T], U8, name="xs_win", offset=15872)
         nc.vector.memset(xs_win[:, 0 : T // 2].bitcast(I32), 0)
         nc.gpsimd.memset(xs_win[:, T // 2 : T].bitcast(I32), 0)
+        w2w_raw = keep.tile([P, H], I32, name="w2w_raw")
+        nc.sync.dma_start(w2w_raw[:], w2_words[0].rearrange("p n t -> p (n t)").bitcast(I32))
         w2s_raw = keep.tile([P, H], U8, name="w2s_raw")
         for q in range(4):
-            nc.sync.dma_start(
+            eng = nc.sync if q < 2 else nc.scalar
+            eng.dma_start(
                 w2s_raw[32 * q : 32 * q + 32, :].bitcast(I32),
                 w2_scales[0, 4 * q : 4 * q + 4, :].bitcast(I32).unsqueeze(0).to_broadcast([8, 4, H // 4]),
             )
@@ -68,18 +70,28 @@ def tile_picked_phpq_gelu_po_kernel(
             nc.sync.dma_start(raw[:], w1_rows[:, :, a * piece : (a + 1) * piece])
             w1_raw.append(raw)
 
-        w2w_raw = keep.tile([P, H], I32, name="w2w_raw")
-        nc.sync.dma_start(w2w_raw[:], w2_words[0].rearrange("p n t -> p (n t)").bitcast(I32))
+        pos_rows = pos.rearrange("(p t) s -> p t s", t=PACK)
+        pos_head = keep.tile([P, PACK, UNIT], F32, name="pos_head")
+        nc.sync.dma_start(pos_head[:], pos_rows[:, :, 0:UNIT])
 
         xs_plane = keep.tile([P, S], U8, name="xs_plane", align_bytes=64)
         nc.vector.memset(xs_plane[:].bitcast(I32), 0)
 
-        pos_rows = pos.rearrange("(p t) s -> p t s", t=PACK)
         pos_sb = shared.tile([P, PACK, S], F32, name="pos_sb", offset=0)
 
         def load_pos(i):
             a, b = POS_PIECES[i]
             nc.sync.dma_start(pos_sb[:, :, a:b], pos_rows[:, :, a:b])
+
+        w2_q = keep.tile([P, H], I32, name="w2_q", align_bytes=64)
+        w2_s = keep.tile([P, H], U8, name="w2_s", align_bytes=64)
+        nc.vector.tensor_copy(
+            w2_q[:].rearrange("p (t b i) -> p b t i", t=PACK, i=4),
+            w2w_raw[:].rearrange("p (b i t) -> p b t i", t=PACK, i=4),
+        )
+        nc.vector.tensor_copy(
+            w2_s[:].rearrange("p (t m) -> p t m", t=PACK), w2s_raw[:].rearrange("p (m t) -> p t m", t=PACK)
+        )
 
         xs_got = keep.tile([P, S], U8, name="xs_got")
         nc.vector.tensor_copy(xs_got[:], xs_win[:].indirect(offsets[:]))
@@ -116,18 +128,6 @@ def tile_picked_phpq_gelu_po_kernel(
 
         xq_late = shared.tile([P, S - EARLY], U32, name="xq_late", align_bytes=64, offset=20992)
         nc.vector.tensor_copy(xq_late[:], xw_win[:].indirect(offsets[:, EARLY // 16 : S // 16]))
-
-        w2_q = shared.tile([P, H], I32, name="w2_q", align_bytes=64, offset=18432)
-        w2_s = shared.tile([P, H], U8, name="w2_s", align_bytes=64, offset=20480)
-
-        def deal_w2():
-            nc.vector.tensor_copy(
-                w2_s[:].rearrange("p (t m) -> p t m", t=PACK), w2s_raw[:].rearrange("p (m t) -> p t m", t=PACK)
-            )
-            nc.vector.tensor_copy(
-                w2_q[:].rearrange("p (t b i) -> p b t i", t=PACK, i=4),
-                w2w_raw[:].rearrange("p (b i t) -> p b t i", t=PACK, i=4),
-            )
 
         out_q = keep.tile([P, S], U32, name="out_q", align_bytes=64)
         out_s = keep.tile([P, S], U8, name="out_s", align_bytes=64)
@@ -166,7 +166,7 @@ def tile_picked_phpq_gelu_po_kernel(
             codes = xq_early[:, cols] if u < early else xq_late[:, columns(u - early, u - early + 1)]
             bank = product("acc1", w1_q, w1_s, codes, xs_plane[:, cols])
             pre = keep.tile([P, PACK, UNIT], F32, name=f"pre{u}")
-            nc.vector.tensor_tensor(pre[:], bank[:], pos_sb[:, :, cols], ADD)
+            nc.vector.tensor_tensor(pre[:], bank[:], pos_head[:] if u == 0 else pos_sb[:, :, cols], ADD)
             h_bf[u] = keep.tile([P, UNIT, PACK], BF16, name=f"h_bf{u}", align_bytes=64)
             nc.scalar.activation(
                 h_bf[u][:].rearrange("p (g i) t -> p g t i", i=2),
@@ -208,14 +208,12 @@ def tile_picked_phpq_gelu_po_kernel(
         for step in range(N_UNITS + COPY_LAG):
             if step < N_UNITS:
                 layer1(step)
-            if step == 0:
-                deal_w2()
             if 0 <= step - 1 < N_UNITS:
                 layer2(step - 1)
             if 0 <= step - COPY_LAG < N_UNITS:
                 leave(step - COPY_LAG)
-        for a, b in PLANE_GROUPS:
-            planes(a, b)
+        for u in range(N_UNITS):
+            planes(u, u + 1)
 
         for q in range(4):
             eng = nc.sync if q % 2 == 0 else nc.scalar

@@ -42,16 +42,16 @@ def tile_picked_phpq_gelu_po_kernel(
         nc.sync.dma_start(offsets[:], offs)
 
         xs_win = shared.tile([P, T], U8, name="xs_win", offset=15872)
+        w2s_raw = keep.tile([P, H], U8, name="w2s_raw")
+        nc.vector.memset(w2s_raw[:].bitcast(I32), 0)
         nc.vector.memset(xs_win[:, 0 : T // 2].bitcast(I32), 0)
         nc.gpsimd.memset(xs_win[:, T // 2 : T].bitcast(I32), 0)
         w2w_raw = keep.tile([P, H], I32, name="w2w_raw")
         nc.sync.dma_start(w2w_raw[:], w2_words[0].rearrange("p n t -> p (n t)").bitcast(I32))
-        w2s_raw = keep.tile([P, H], U8, name="w2s_raw")
         for q in range(4):
             eng = nc.sync if q < 2 else nc.scalar
             eng.dma_start(
-                w2s_raw[32 * q : 32 * q + 32, :].bitcast(I32),
-                w2_scales[0, 4 * q : 4 * q + 4, :].bitcast(I32).unsqueeze(0).to_broadcast([8, 4, H // 4]),
+                w2s_raw[32 * q : 32 * q + 4, :].bitcast(I32), w2_scales[0, 4 * q : 4 * q + 4, :].bitcast(I32)
             )
         nc.sync.dma_start(xs_win[0:P:8, :].bitcast(I32), x_scales[0].bitcast(I32))
         warm = keep.tile([P, 1], F32, name="warm")
@@ -190,19 +190,23 @@ def tile_picked_phpq_gelu_po_kernel(
                 if g1 == u + 1:
                     nc.sync.dma_start(out_rows[:, :, columns(g0, g1)], tile[:])
 
-        def planes(a, b):
-            cols = columns(a, b)
-            tile, first = y[a]
-            y_bf = keep.tile([P, (b - a) * UNIT, PACK], BF16, name=f"y_bf{a}", align_bytes=64)
+        y_bf = {}
+
+        def round_y(u):
+            tile, first = y[u]
+            y_bf[u] = keep.tile([P, UNIT, PACK], BF16, name=f"y_bf{u}", align_bytes=64)
             nc.vector.tensor_copy(
-                y_bf[:].rearrange("p (g i) t -> p g t i", i=2),
-                tile[:, :, columns(a - first, b - first)].rearrange("p t (g i) -> p g t i", i=2),
+                y_bf[u][:].rearrange("p (g i) t -> p g t i", i=2),
+                tile[:, :, columns(u - first, u - first + 1)].rearrange("p t (g i) -> p g t i", i=2),
             )
+
+        def quantize_y(u):
+            cols = columns(u, u + 1)
             nc.vector.quantize_mx(
-                out=out_q[:, cols].bitcast(FP8X4), scales=out_s[:, cols], in_=y_bf[:].rearrange("p n t -> p (n t)")
+                out=out_q[:, cols].bitcast(FP8X4), scales=out_s[:, cols], in_=y_bf[u][:].rearrange("p n t -> p (n t)")
             )
             for g0, g1 in WORD_GROUPS:
-                if g1 == b:
+                if g1 == u + 1:
                     nc.sync.dma_start(out_words[:, columns(g0, g1)], out_q[:, columns(g0, g1)].bitcast(I32))
 
         for step in range(N_UNITS + COPY_LAG):
@@ -212,8 +216,11 @@ def tile_picked_phpq_gelu_po_kernel(
                 layer2(step - 1)
             if 0 <= step - COPY_LAG < N_UNITS:
                 leave(step - COPY_LAG)
-        for u in range(N_UNITS):
-            planes(u, u + 1)
+        for u in range(N_UNITS + 1):
+            if u < N_UNITS:
+                round_y(u)
+            if u >= 1:
+                quantize_y(u - 1)
 
         for q in range(4):
             eng = nc.sync if q % 2 == 0 else nc.scalar

@@ -20,7 +20,7 @@ PACK = 4
 UNIT = 128
 N_UNITS = S // UNIT
 EARLY = 768
-OUT_GROUPS = ((0, 1), (1, 3), (3, 5), (5, 6), (6, 8))
+OUT_GROUPS = ((0, 1), (1, 3), (3, 4), (4, 5), (5, 6), (6, 8))
 WORD_GROUPS = ((0, 2), (2, 4), (4, 6), (6, 8))
 COPY_LAG = 2
 VECTOR_COPIES = (1,)
@@ -130,7 +130,7 @@ def tile_picked_phpq_gelu_po_kernel(
         nc.vector.tensor_copy(xq_late[:], xw_win[:].indirect(offsets[:, EARLY // 16 : S // 16]))
 
         out_q = keep.tile([P, S], U32, name="out_q", align_bytes=64)
-        out_s = keep.tile([P, S], U8, name="out_s", align_bytes=64)
+        out_s = keep.tile([P, S // 4], U8, name="out_s", align_bytes=64)
         out_rows = out_0.rearrange("(p t) s -> p t s", t=PACK)
         out_words = out_1[0].rearrange("p n t -> p (n t)").bitcast(I32)
 
@@ -203,7 +203,9 @@ def tile_picked_phpq_gelu_po_kernel(
         def quantize_y(u):
             cols = columns(u, u + 1)
             nc.vector.quantize_mx(
-                out=out_q[:, cols].bitcast(FP8X4), scales=out_s[:, cols], in_=y_bf[u][:].rearrange("p n t -> p (n t)")
+                out=out_q[:, cols].bitcast(FP8X4),
+                scales=out_s[4 * (u // 2) : P, columns(u % 2, u % 2 + 1)],
+                in_=y_bf[u][:].rearrange("p n t -> p (n t)"),
             )
             for g0, g1 in WORD_GROUPS:
                 if g1 == u + 1:
@@ -224,4 +226,7 @@ def tile_picked_phpq_gelu_po_kernel(
 
         for q in range(4):
             eng = nc.sync if q % 2 == 0 else nc.scalar
-            eng.dma_start(out_2[0, 4 * q : 4 * q + 4, :].bitcast(I32), out_s[32 * q : 32 * q + 4, :].bitcast(I32))
+            eng.dma_start(
+                out_2[0, 4 * q : 4 * q + 4, :].bitcast(I32).rearrange("c (g n) -> g c n", g=4),
+                out_s[32 * q : 32 * q + 16, :].bitcast(I32),
+            )

@@ -24,7 +24,7 @@ OUT_GROUPS = ((0, 1), (1, 3), (3, 4), (4, 5), (5, 6), (6, 8))
 WORD_GROUPS = ((0, 2), (2, 4), (4, 6), (6, 8))
 COPY_LAG = 2
 VECTOR_COPIES = (1,)
-W1_VECTOR_M = 80
+W1_SCALAR_M = 104
 W1_PIECES = 1
 POS_PIECES = ((128, 384), (384, 640), (640, 896), (896, 1024))
 
@@ -106,16 +106,16 @@ def tile_picked_phpq_gelu_po_kernel(
         nc.vector.tensor_copy(xq_early[:], xw_win[:].indirect(offsets[:, 0 : EARLY // 16]))
 
         w1_bf = shared.tile([P, PACK, P, PACK], BF16, name="w1_bf", align_bytes=64, offset=18432)
-        ms = piece // PACK
 
-        def round_w1(copy, a, m0, m1):
+        def round_w1(copy, s, m0, m1):
             copy(
-                w1_bf[:, :, a * ms + m0 : a * ms + m1, :].rearrange("p (s e) m j -> p m s j e", e=2),
-                w1_raw[a][:, :, PACK * m0 : PACK * m1].rearrange("p j (m s e) -> p m s j e", s=2, e=2),
+                w1_bf[:, 2 * s : 2 * s + 2, m0:m1, :].rearrange("p e m j -> p m j e"),
+                w1_raw[0][:].rearrange("p j (m t) -> p m j t", t=PACK)[:, m0:m1, :, 2 * s : 2 * s + 2],
             )
 
-        round_w1(nc.vector.tensor_copy, 0, 0, W1_VECTOR_M)
-        round_w1(nc.scalar.copy, 0, W1_VECTOR_M, ms)
+        round_w1(nc.vector.tensor_copy, 0, 0, P)
+        round_w1(nc.scalar.copy, 1, 0, W1_SCALAR_M)
+        round_w1(nc.vector.tensor_copy, 1, W1_SCALAR_M, P)
         w1_q = keep.tile([P, H], U32, name="w1_q", align_bytes=64)
         w1_s = keep.tile([P, H], U8, name="w1_s", align_bytes=64)
         for t in range(PACK):

@@ -17,16 +17,22 @@ ADD = mybir.AluOpType.add
 
 P = 128
 PACK = 4
+QUADRANTS = 4
 UNIT = 128
 N_UNITS = S // UNIT
+BANKS = 4
+
 EARLY = 768
-OUT_GROUPS = ((0, 1), (1, 3), (3, 4), (4, 5), (5, 6), (6, 8))
-WORD_GROUPS = ((0, 2), (2, 4), (4, 6), (6, 8))
+W1_SCALAR_GROUPS = 104
+VECTOR_COPY_UNIT = 1
 COPY_LAG = 2
-VECTOR_COPIES = (1,)
-W1_SCALAR_M = 104
-W1_PIECES = 1
-POS_PIECES = ((128, 384), (384, 640), (640, 896), (896, 1024))
+POS_PIECES = ((128, 384), (384, 512), (512, 768), (768, 1024))
+OUT_GROUPS = ((0, 1), (1, 3), (3, 4), (4, 5), (5, 6), (6, 8))
+
+POS_BYTES = PACK * S * 4
+XS_WIN_AT = POS_BYTES - 512
+W1_BF_AT = POS_BYTES + T
+XQ_LATE_AT = W1_BF_AT + 2560
 
 
 def tile_picked_phpq_gelu_po_kernel(
@@ -36,24 +42,26 @@ def tile_picked_phpq_gelu_po_kernel(
     with ExitStack() as ctx:
         keep = ctx.enter_context(tc.tile_pool(name="keep", bufs=1))
         shared = ctx.enter_context(tc.tile_pool(name="shared", bufs=1))
-        psum = ctx.enter_context(tc.psum_pool(name="psum", bufs=4))
+        psum = ctx.enter_context(tc.psum_pool(name="psum", bufs=BANKS))
 
         offsets = keep.tile([P, S // 16], U16, name="offsets")
         nc.sync.dma_start(offsets[:], offs)
 
-        xs_win = shared.tile([P, T], U8, name="xs_win", offset=15872)
+        xs_win = shared.tile([P, T], U8, name="xs_win", offset=XS_WIN_AT)
         w2s_raw = keep.tile([P, H], U8, name="w2s_raw")
         nc.vector.memset(w2s_raw[:].bitcast(I32), 0)
         nc.vector.memset(xs_win[:, 0 : T // 2].bitcast(I32), 0)
         nc.gpsimd.memset(xs_win[:, T // 2 : T].bitcast(I32), 0)
+
         w2w_raw = keep.tile([P, H], I32, name="w2w_raw")
         nc.sync.dma_start(w2w_raw[:], w2_words[0].rearrange("p n t -> p (n t)").bitcast(I32))
-        for q in range(4):
-            eng = nc.sync if q < 2 else nc.scalar
+        for q in range(QUADRANTS):
+            eng = nc.sync if q < QUADRANTS // 2 else nc.scalar
             eng.dma_start(
                 w2s_raw[32 * q : 32 * q + 4, :].bitcast(I32), w2_scales[0, 4 * q : 4 * q + 4, :].bitcast(I32)
             )
         nc.sync.dma_start(xs_win[0:P:8, :].bitcast(I32), x_scales[0].bitcast(I32))
+
         warm = keep.tile([P, 1], F32, name="warm")
         nc.vector.memset(warm[:], 0.0)
         warm_out = keep.tile([P, 1], F32, name="warm_out")
@@ -62,13 +70,8 @@ def tile_picked_phpq_gelu_po_kernel(
         xw_win = keep.tile([P, T], U32, name="xw_win")
         nc.sync.dma_start(xw_win[:].bitcast(I32), x_words[0].rearrange("p n t -> p (n t)").bitcast(I32))
 
-        w1_rows = w1.rearrange("(p j) c -> p j c", j=PACK)
-        piece = H // W1_PIECES
-        w1_raw = []
-        for a in range(W1_PIECES):
-            raw = keep.tile([P, PACK, piece], F32, name=f"w1_raw{a}")
-            nc.sync.dma_start(raw[:], w1_rows[:, :, a * piece : (a + 1) * piece])
-            w1_raw.append(raw)
+        w1_raw = keep.tile([P, PACK, H], F32, name="w1_raw0")
+        nc.sync.dma_start(w1_raw[:], w1.rearrange("(p j) c -> p j c", j=PACK))
 
         pos_rows = pos.rearrange("(p t) s -> p t s", t=PACK)
         pos_head = keep.tile([P, PACK, UNIT], F32, name="pos_head")
@@ -78,10 +81,6 @@ def tile_picked_phpq_gelu_po_kernel(
         nc.vector.memset(xs_plane[:].bitcast(I32), 0)
 
         pos_sb = shared.tile([P, PACK, S], F32, name="pos_sb", offset=0)
-
-        def load_pos(i):
-            a, b = POS_PIECES[i]
-            nc.sync.dma_start(pos_sb[:, :, a:b], pos_rows[:, :, a:b])
 
         w2_q = keep.tile([P, H], I32, name="w2_q", align_bytes=64)
         w2_s = keep.tile([P, H], U8, name="w2_s", align_bytes=64)
@@ -95,27 +94,27 @@ def tile_picked_phpq_gelu_po_kernel(
 
         xs_got = keep.tile([P, S], U8, name="xs_got")
         nc.vector.tensor_copy(xs_got[:], xs_win[:].indirect(offsets[:]))
-        for q in range(4):
-            nc.sync.dma_start(xs_plane[32 * q : 32 * q + 4, :].bitcast(I32), xs_got[32 * q : 32 * q + 32 : 8, :].bitcast(I32))
-        load_pos(0)
-        load_pos(1)
-        load_pos(2)
-        load_pos(3)
+        for q in range(QUADRANTS):
+            nc.sync.dma_start(
+                xs_plane[32 * q : 32 * q + 4, :].bitcast(I32), xs_got[32 * q : 32 * q + 32 : 8, :].bitcast(I32)
+            )
+        for a, b in POS_PIECES:
+            nc.sync.dma_start(pos_sb[:, :, a:b], pos_rows[:, :, a:b])
 
         xq_early = keep.tile([P, EARLY], U32, name="xq_early", align_bytes=64)
         nc.vector.tensor_copy(xq_early[:], xw_win[:].indirect(offsets[:, 0 : EARLY // 16]))
 
-        w1_bf = shared.tile([P, PACK, P, PACK], BF16, name="w1_bf", align_bytes=64, offset=18432)
+        w1_bf = shared.tile([P, PACK, P, PACK], BF16, name="w1_bf", align_bytes=64, offset=W1_BF_AT)
 
         def round_w1(copy, s, m0, m1):
             copy(
                 w1_bf[:, 2 * s : 2 * s + 2, m0:m1, :].rearrange("p e m j -> p m j e"),
-                w1_raw[0][:].rearrange("p j (m t) -> p m j t", t=PACK)[:, m0:m1, :, 2 * s : 2 * s + 2],
+                w1_raw[:].rearrange("p j (m t) -> p m j t", t=PACK)[:, m0:m1, :, 2 * s : 2 * s + 2],
             )
 
         round_w1(nc.vector.tensor_copy, 0, 0, P)
-        round_w1(nc.scalar.copy, 1, 0, W1_SCALAR_M)
-        round_w1(nc.vector.tensor_copy, 1, W1_SCALAR_M, P)
+        round_w1(nc.scalar.copy, 1, 0, W1_SCALAR_GROUPS)
+        round_w1(nc.vector.tensor_copy, 1, W1_SCALAR_GROUPS, P)
         w1_q = keep.tile([P, H], U32, name="w1_q", align_bytes=64)
         w1_s = keep.tile([P, H], U8, name="w1_s", align_bytes=64)
         for t in range(PACK):
@@ -126,11 +125,11 @@ def tile_picked_phpq_gelu_po_kernel(
                 in_=w1_bf[:, t, :, :].rearrange("p m j -> p (m j)"),
             )
 
-        xq_late = shared.tile([P, S - EARLY], U32, name="xq_late", align_bytes=64, offset=20992)
+        xq_late = shared.tile([P, S - EARLY], U32, name="xq_late", align_bytes=64, offset=XQ_LATE_AT)
         nc.vector.tensor_copy(xq_late[:], xw_win[:].indirect(offsets[:, EARLY // 16 : S // 16]))
 
         out_q = keep.tile([P, S], U32, name="out_q", align_bytes=64)
-        out_s = keep.tile([P, S // 4], U8, name="out_s", align_bytes=64)
+        out_s = keep.tile([P, 2 * UNIT], U8, name="out_s", align_bytes=64)
         out_rows = out_0.rearrange("(p t) s -> p t s", t=PACK)
         out_words = out_1[0].rearrange("p n t -> p (n t)").bitcast(I32)
 
@@ -155,6 +154,7 @@ def tile_picked_phpq_gelu_po_kernel(
         h_bf = {}
         acc2 = {}
         y = {}
+        y_bf = {}
         for a, b in OUT_GROUPS:
             tile = keep.tile([P, PACK, (b - a) * UNIT], F32, name=f"y{a}")
             for u in range(a, b):
@@ -183,14 +183,11 @@ def tile_picked_phpq_gelu_po_kernel(
             acc2[u] = product("acc2", w2_q, w2_s, h_q[:], h_s[:])
 
         def leave(u):
-            tile, a = y[u]
-            copy = nc.vector.tensor_copy if u in VECTOR_COPIES else nc.scalar.copy
-            copy(tile[:, :, columns(u - a, u - a + 1)], acc2[u][:])
-            for g0, g1 in OUT_GROUPS:
-                if g1 == u + 1:
-                    nc.sync.dma_start(out_rows[:, :, columns(g0, g1)], tile[:])
-
-        y_bf = {}
+            tile, first = y[u]
+            copy = nc.vector.tensor_copy if u == VECTOR_COPY_UNIT else nc.scalar.copy
+            copy(tile[:, :, columns(u - first, u - first + 1)], acc2[u][:])
+            if (first, u + 1) in OUT_GROUPS:
+                nc.sync.dma_start(out_rows[:, :, columns(first, u + 1)], tile[:])
 
         def round_y(u):
             tile, first = y[u]
@@ -201,32 +198,32 @@ def tile_picked_phpq_gelu_po_kernel(
             )
 
         def quantize_y(u):
-            cols = columns(u, u + 1)
             nc.vector.quantize_mx(
-                out=out_q[:, cols].bitcast(FP8X4),
+                out=out_q[:, columns(u, u + 1)].bitcast(FP8X4),
                 scales=out_s[4 * (u // 2) : P, columns(u % 2, u % 2 + 1)],
                 in_=y_bf[u][:].rearrange("p n t -> p (n t)"),
             )
-            for g0, g1 in WORD_GROUPS:
-                if g1 == u + 1:
-                    nc.sync.dma_start(out_words[:, columns(g0, g1)], out_q[:, columns(g0, g1)].bitcast(I32))
+            if u % 2 == 1:
+                pair = columns(u - 1, u + 1)
+                nc.sync.dma_start(out_words[:, pair], out_q[:, pair].bitcast(I32))
 
         for step in range(N_UNITS + COPY_LAG):
             if step < N_UNITS:
                 layer1(step)
             if 0 <= step - 1 < N_UNITS:
                 layer2(step - 1)
-            if 0 <= step - COPY_LAG < N_UNITS:
+            if 0 <= step - COPY_LAG:
                 leave(step - COPY_LAG)
+
         for u in range(N_UNITS + 1):
             if u < N_UNITS:
                 round_y(u)
             if u >= 1:
                 quantize_y(u - 1)
 
-        for q in range(4):
+        for q in range(QUADRANTS):
             eng = nc.sync if q % 2 == 0 else nc.scalar
             eng.dma_start(
-                out_2[0, 4 * q : 4 * q + 4, :].bitcast(I32).rearrange("c (g n) -> g c n", g=4),
+                out_2[0, 4 * q : 4 * q + 4, :].bitcast(I32).rearrange("c (g n) -> g c n", g=N_UNITS // 2),
                 out_s[32 * q : 32 * q + 16, :].bitcast(I32),
             )

@@ -49,15 +49,14 @@ def tile_picked_phpq_gelu_po_kernel(
 
         xs_win = shared.tile([P, T], U8, name="xs_win", offset=XS_WIN_AT)
         w2s_raw = keep.tile([P, H], U8, name="w2s_raw")
+        nc.vector.memset(xs_win[:, 0 : 3 * T // 4].bitcast(I32), 0)
+        nc.gpsimd.memset(xs_win[:, 3 * T // 4 : T].bitcast(I32), 0)
         nc.vector.memset(w2s_raw[:].bitcast(I32), 0)
-        nc.vector.memset(xs_win[:, 0 : T // 2].bitcast(I32), 0)
-        nc.gpsimd.memset(xs_win[:, T // 2 : T].bitcast(I32), 0)
 
         w2w_raw = keep.tile([P, H], I32, name="w2w_raw")
         nc.sync.dma_start(w2w_raw[:], w2_words[0].rearrange("p n t -> p (n t)").bitcast(I32))
         for q in range(QUADRANTS):
-            eng = nc.sync if q < QUADRANTS // 2 else nc.scalar
-            eng.dma_start(
+            nc.scalar.dma_start(
                 w2s_raw[32 * q : 32 * q + 4, :].bitcast(I32), w2_scales[0, 4 * q : 4 * q + 4, :].bitcast(I32)
             )
         nc.sync.dma_start(xs_win[0:P:8, :].bitcast(I32), x_scales[0].bitcast(I32))
@@ -84,11 +83,11 @@ def tile_picked_phpq_gelu_po_kernel(
 
         w2_q = keep.tile([P, H], I32, name="w2_q", align_bytes=64)
         w2_s = keep.tile([P, H], U8, name="w2_s", align_bytes=64)
-        nc.vector.tensor_copy(
+        nc.gpsimd.tensor_copy(
             w2_q[:].rearrange("p (t b i) -> p b t i", t=PACK, i=4),
             w2w_raw[:].rearrange("p (b i t) -> p b t i", t=PACK, i=4),
         )
-        nc.vector.tensor_copy(
+        nc.gpsimd.tensor_copy(
             w2_s[:].rearrange("p (t m) -> p t m", t=PACK), w2s_raw[:].rearrange("p (m t) -> p t m", t=PACK)
         )
 
@@ -101,8 +100,8 @@ def tile_picked_phpq_gelu_po_kernel(
         for a, b in POS_PIECES:
             nc.sync.dma_start(pos_sb[:, :, a:b], pos_rows[:, :, a:b])
 
-        xq_early = keep.tile([P, EARLY], U32, name="xq_early", align_bytes=64)
-        nc.vector.tensor_copy(xq_early[:], xw_win[:].indirect(offsets[:, 0 : EARLY // 16]))
+        xq = keep.tile([P, S], U32, name="xq", align_bytes=64)
+        nc.vector.tensor_copy(xq[:], xw_win[:].indirect(offsets[:]))
 
         w1_bf = shared.tile([P, PACK, P, PACK], BF16, name="w1_bf", align_bytes=64, offset=W1_BF_AT)
 
@@ -124,9 +123,6 @@ def tile_picked_phpq_gelu_po_kernel(
                 scales=w1_s[:, cols],
                 in_=w1_bf[:, t, :, :].rearrange("p m j -> p (m j)"),
             )
-
-        xq_late = shared.tile([P, S - EARLY], U32, name="xq_late", align_bytes=64, offset=XQ_LATE_AT)
-        nc.vector.tensor_copy(xq_late[:], xw_win[:].indirect(offsets[:, EARLY // 16 : S // 16]))
 
         out_q = keep.tile([P, S], U32, name="out_q", align_bytes=64)
         out_s = keep.tile([P, 2 * UNIT], U8, name="out_s", align_bytes=64)
@@ -162,9 +158,7 @@ def tile_picked_phpq_gelu_po_kernel(
 
         def layer1(u):
             cols = columns(u, u + 1)
-            early = EARLY // UNIT
-            codes = xq_early[:, cols] if u < early else xq_late[:, columns(u - early, u - early + 1)]
-            bank = product("acc1", w1_q, w1_s, codes, xs_plane[:, cols])
+            bank = product("acc1", w1_q, w1_s, xq[:, cols], xs_plane[:, cols])
             pre = keep.tile([P, PACK, UNIT], F32, name=f"pre{u}")
             nc.vector.tensor_tensor(pre[:], bank[:], pos_head[:] if u == 0 else pos_sb[:, :, cols], ADD)
             h_bf[u] = keep.tile([P, UNIT, PACK], BF16, name=f"h_bf{u}", align_bytes=64)

@@ -26,7 +26,7 @@ EARLY = 768
 W1_SCALAR_GROUPS = 104
 VECTOR_COPY_UNIT = 1
 COPY_LAG = 2
-POS_PIECES = ((128, 384), (384, 512), (512, 768), (768, 1024))
+POS_PIECES = ((0, 256), (256, 512), (512, 768), (768, 1024))
 OUT_GROUPS = ((0, 1), (1, 3), (3, 4), (4, 5), (5, 6), (6, 8))
 
 POS_BYTES = PACK * S * 4
@@ -44,6 +44,9 @@ def tile_picked_phpq_gelu_po_kernel(
         shared = ctx.enter_context(tc.tile_pool(name="shared", bufs=1))
         psum = ctx.enter_context(tc.psum_pool(name="psum", bufs=BANKS))
 
+        xw_win = keep.tile([P, T], U32, name="xw_win")
+        x_rows = x_words[0].rearrange("p n t -> p (n t)").bitcast(I32)
+        nc.sync.dma_start(xw_win[:, 0 : T // 4].bitcast(I32), x_rows[:, 0 : T // 4])
         offsets = keep.tile([P, S // 16], U16, name="offsets")
         nc.sync.dma_start(offsets[:], offs)
 
@@ -53,8 +56,6 @@ def tile_picked_phpq_gelu_po_kernel(
         nc.gpsimd.memset(xs_win[:, 3 * T // 4 : T].bitcast(I32), 0)
         nc.vector.memset(w2s_raw[:].bitcast(I32), 0)
 
-        w2w_raw = keep.tile([P, H], I32, name="w2w_raw")
-        nc.sync.dma_start(w2w_raw[:], w2_words[0].rearrange("p n t -> p (n t)").bitcast(I32))
         for q in range(QUADRANTS):
             nc.scalar.dma_start(
                 w2s_raw[32 * q : 32 * q + 4, :].bitcast(I32), w2_scales[0, 4 * q : 4 * q + 4, :].bitcast(I32)
@@ -66,27 +67,21 @@ def tile_picked_phpq_gelu_po_kernel(
         warm_out = keep.tile([P, 1], F32, name="warm_out")
         nc.scalar.activation(warm_out[:], warm[:], GELU)
 
-        xw_win = keep.tile([P, T], U32, name="xw_win")
-        nc.sync.dma_start(xw_win[:].bitcast(I32), x_words[0].rearrange("p n t -> p (n t)").bitcast(I32))
+        nc.sync.dma_start(xw_win[:, T // 4 : T].bitcast(I32), x_rows[:, T // 4 : T])
 
         w1_raw = keep.tile([P, PACK, H], F32, name="w1_raw0")
         nc.sync.dma_start(w1_raw[:], w1.rearrange("(p j) c -> p j c", j=PACK))
 
         pos_rows = pos.rearrange("(p t) s -> p t s", t=PACK)
-        pos_head = keep.tile([P, PACK, UNIT], F32, name="pos_head")
-        nc.sync.dma_start(pos_head[:], pos_rows[:, :, 0:UNIT])
+        w2w_raw = keep.tile([P, H], I32, name="w2w_raw")
+        nc.sync.dma_start(w2w_raw[:], w2_words[0].rearrange("p n t -> p (n t)").bitcast(I32))
 
         xs_plane = keep.tile([P, S], U8, name="xs_plane", align_bytes=64)
         nc.vector.memset(xs_plane[:].bitcast(I32), 0)
 
         pos_sb = shared.tile([P, PACK, S], F32, name="pos_sb", offset=0)
 
-        w2_q = keep.tile([P, H], I32, name="w2_q", align_bytes=64)
         w2_s = keep.tile([P, H], U8, name="w2_s", align_bytes=64)
-        nc.gpsimd.tensor_copy(
-            w2_q[:].rearrange("p (t b i) -> p b t i", t=PACK, i=4),
-            w2w_raw[:].rearrange("p (b i t) -> p b t i", t=PACK, i=4),
-        )
         nc.gpsimd.tensor_copy(
             w2_s[:].rearrange("p (t m) -> p t m", t=PACK), w2s_raw[:].rearrange("p (m t) -> p t m", t=PACK)
         )
@@ -100,8 +95,8 @@ def tile_picked_phpq_gelu_po_kernel(
         for a, b in POS_PIECES:
             nc.sync.dma_start(pos_sb[:, :, a:b], pos_rows[:, :, a:b])
 
-        xq = keep.tile([P, S], U32, name="xq", align_bytes=64)
-        nc.vector.tensor_copy(xq[:], xw_win[:].indirect(offsets[:]))
+        xq_early = keep.tile([P, EARLY], U32, name="xq_early", align_bytes=64)
+        nc.vector.tensor_copy(xq_early[:], xw_win[:].indirect(offsets[:, 0 : EARLY // 16]))
 
         w1_bf = shared.tile([P, PACK, P, PACK], BF16, name="w1_bf", align_bytes=64, offset=W1_BF_AT)
 
@@ -123,6 +118,14 @@ def tile_picked_phpq_gelu_po_kernel(
                 scales=w1_s[:, cols],
                 in_=w1_bf[:, t, :, :].rearrange("p m j -> p (m j)"),
             )
+
+        xq_late = shared.tile([P, S - EARLY], U32, name="xq_late", align_bytes=64, offset=XQ_LATE_AT)
+        nc.vector.tensor_copy(xq_late[:], xw_win[:].indirect(offsets[:, EARLY // 16 : S // 16]))
+        w2_q = shared.tile([P, H], I32, name="w2_q", align_bytes=64, offset=W1_BF_AT)
+        nc.gpsimd.tensor_copy(
+            w2_q[:].rearrange("p (t b i) -> p b t i", t=PACK, i=4),
+            w2w_raw[:].rearrange("p (b i t) -> p b t i", t=PACK, i=4),
+        )
 
         out_q = keep.tile([P, S], U32, name="out_q", align_bytes=64)
         out_s = keep.tile([P, 2 * UNIT], U8, name="out_s", align_bytes=64)
@@ -158,9 +161,11 @@ def tile_picked_phpq_gelu_po_kernel(
 
         def layer1(u):
             cols = columns(u, u + 1)
-            bank = product("acc1", w1_q, w1_s, xq[:, cols], xs_plane[:, cols])
+            early = EARLY // UNIT
+            codes = xq_early[:, cols] if u < early else xq_late[:, columns(u - early, u - early + 1)]
+            bank = product("acc1", w1_q, w1_s, codes, xs_plane[:, cols])
             pre = keep.tile([P, PACK, UNIT], F32, name=f"pre{u}")
-            nc.vector.tensor_tensor(pre[:], bank[:], pos_head[:] if u == 0 else pos_sb[:, :, cols], ADD)
+            nc.vector.tensor_tensor(pre[:], bank[:], pos_sb[:, :, cols], ADD)
             h_bf[u] = keep.tile([P, UNIT, PACK], BF16, name=f"h_bf{u}", align_bytes=64)
             nc.scalar.activation(
                 h_bf[u][:].rearrange("p (g i) t -> p g t i", i=2),

@@ -14,6 +14,7 @@ U8 = mybir.dt.uint8
 FP8X4 = mybir.dt.float8_e4m3fn_x4
 GELU = mybir.ActivationFunctionType.Gelu_apprx_tanh
 ADD = mybir.AluOpType.add
+MULT = mybir.AluOpType.mult
 
 P = 128
 PACK = 4
@@ -33,6 +34,8 @@ POS_BYTES = PACK * S * 4
 XS_WIN_AT = POS_BYTES - 512
 W1_BF_AT = POS_BYTES + T
 XQ_LATE_AT = W1_BF_AT + 2560
+H_BF_AT = W1_BF_AT + 4096
+GPSIMD_BEHIND = {0: 2, 1: 4}
 
 
 def tile_picked_phpq_gelu_po_kernel(
@@ -150,6 +153,7 @@ def tile_picked_phpq_gelu_po_kernel(
                 )
             return bank
 
+        pres = {}
         h_bf = {}
         acc2 = {}
         y = {}
@@ -166,7 +170,11 @@ def tile_picked_phpq_gelu_po_kernel(
             bank = product("acc1", w1_q, w1_s, codes, xs_plane[:, cols])
             pre = keep.tile([P, PACK, UNIT], F32, name=f"pre{u}")
             nc.vector.tensor_tensor(pre[:], bank[:], pos_sb[:, :, cols], ADD)
-            h_bf[u] = keep.tile([P, UNIT, PACK], BF16, name=f"h_bf{u}", align_bytes=64)
+            pres[u] = pre
+
+        def gelu(u):
+            pre = pres[u]
+            h_bf[u] = shared.tile([P, UNIT, PACK], BF16, name=f"h_bf{u}", align_bytes=64, offset=H_BF_AT + u * 1024)
             nc.scalar.activation(
                 h_bf[u][:].rearrange("p (g i) t -> p g t i", i=2),
                 pre[:].rearrange("p t (g i) -> p g t i", i=2),
@@ -190,11 +198,14 @@ def tile_picked_phpq_gelu_po_kernel(
 
         def round_y(u):
             tile, first = y[u]
-            y_bf[u] = keep.tile([P, UNIT, PACK], BF16, name=f"y_bf{u}", align_bytes=64)
-            nc.vector.tensor_copy(
-                y_bf[u][:].rearrange("p (g i) t -> p g t i", i=2),
-                tile[:, :, columns(u - first, u - first + 1)].rearrange("p t (g i) -> p g t i", i=2),
-            )
+            src = tile[:, :, columns(u - first, u - first + 1)].rearrange("p t (g i) -> p g t i", i=2)
+            if u in GPSIMD_BEHIND:
+                at = H_BF_AT + GPSIMD_BEHIND[u] * 1024
+                y_bf[u] = shared.tile([P, UNIT, PACK], BF16, name=f"y_bf{u}", align_bytes=64, offset=at)
+                nc.gpsimd.tensor_scalar(y_bf[u][:].rearrange("p (g i) t -> p g t i", i=2), src, 1.0, 0.0, MULT, ADD)
+            else:
+                y_bf[u] = keep.tile([P, UNIT, PACK], BF16, name=f"y_bf{u}", align_bytes=64)
+                nc.vector.tensor_copy(y_bf[u][:].rearrange("p (g i) t -> p g t i", i=2), src)
 
         def quantize_y(u):
             nc.vector.quantize_mx(
@@ -206,13 +217,32 @@ def tile_picked_phpq_gelu_po_kernel(
                 pair = columns(u - 1, u + 1)
                 nc.sync.dma_start(out_words[:, pair], out_q[:, pair].bitcast(I32))
 
-        for step in range(N_UNITS + COPY_LAG):
-            if step < N_UNITS:
-                layer1(step)
-            if 0 <= step - 1 < N_UNITS:
-                layer2(step - 1)
-            if 0 <= step - COPY_LAG:
-                leave(step - COPY_LAG)
+        for u in range(3):
+            layer1(u)
+            gelu(u)
+        layer2(0)
+        leave(0)
+        layer1(3)
+        gelu(3)
+        layer2(1)
+        layer2(2)
+        layer1(4)
+        gelu(4)
+        leave(1)
+        layer1(5)
+        leave(2)
+        gelu(5)
+        layer2(3)
+        layer2(4)
+        leave(3)
+        layer1(6)
+        layer1(7)
+        gelu(6)
+        leave(4)
+        gelu(7)
+        for u in range(5, 8):
+            layer2(u)
+            leave(u)
 
         for u in range(N_UNITS + 1):
             if u < N_UNITS:

@@ -23,19 +23,22 @@ UNIT = 128
 N_UNITS = S // UNIT
 BANKS = 4
 
+X_FIRST = T // 4
+XS_VECTOR = 3 * T // 4
 EARLY = 768
 W1_SCALAR_GROUPS = 104
-VECTOR_COPY_UNIT = 1
-COPY_LAG = 2
-POS_PIECES = ((0, 256), (256, 512), (512, 768), (768, 1024))
+POS_PIECE = 2 * UNIT
+VECTOR_COPY_UNITS = (1, 4)
+GPSIMD_BEHIND = {0: 2, 1: 4}
 OUT_GROUPS = ((0, 1), (1, 3), (3, 4), (4, 5), (5, 6), (6, 8))
+WORD_GROUPS = ((0, 3), (3, 6), (6, 8))
 
 POS_BYTES = PACK * S * 4
 XS_WIN_AT = POS_BYTES - 512
 W1_BF_AT = POS_BYTES + T
 XQ_LATE_AT = W1_BF_AT + 2560
-H_BF_AT = W1_BF_AT + 4096
-GPSIMD_BEHIND = {0: 2, 1: 4}
+H_BF_AT = W1_BF_AT + PACK * H * 2
+UNIT_BF_BYTES = PACK * UNIT * 2
 
 
 def tile_picked_phpq_gelu_po_kernel(
@@ -49,14 +52,14 @@ def tile_picked_phpq_gelu_po_kernel(
 
         xw_win = keep.tile([P, T], U32, name="xw_win")
         x_rows = x_words[0].rearrange("p n t -> p (n t)").bitcast(I32)
-        nc.sync.dma_start(xw_win[:, 0 : T // 4].bitcast(I32), x_rows[:, 0 : T // 4])
+        nc.sync.dma_start(xw_win[:, 0:X_FIRST].bitcast(I32), x_rows[:, 0:X_FIRST])
         offsets = keep.tile([P, S // 16], U16, name="offsets")
         nc.sync.dma_start(offsets[:], offs)
 
         xs_win = shared.tile([P, T], U8, name="xs_win", offset=XS_WIN_AT)
         w2s_raw = keep.tile([P, H], U8, name="w2s_raw")
-        nc.vector.memset(xs_win[:, 0 : 3 * T // 4].bitcast(I32), 0)
-        nc.gpsimd.memset(xs_win[:, 3 * T // 4 : T].bitcast(I32), 0)
+        nc.vector.memset(xs_win[:, 0:XS_VECTOR].bitcast(I32), 0)
+        nc.gpsimd.memset(xs_win[:, XS_VECTOR:T].bitcast(I32), 0)
         nc.vector.memset(w2s_raw[:].bitcast(I32), 0)
 
         for q in range(QUADRANTS):
@@ -70,7 +73,7 @@ def tile_picked_phpq_gelu_po_kernel(
         warm_out = keep.tile([P, 1], F32, name="warm_out")
         nc.scalar.activation(warm_out[:], warm[:], GELU)
 
-        nc.sync.dma_start(xw_win[:, T // 4 : T].bitcast(I32), x_rows[:, T // 4 : T])
+        nc.sync.dma_start(xw_win[:, X_FIRST:T].bitcast(I32), x_rows[:, X_FIRST:T])
 
         w1_raw = keep.tile([P, PACK, H], F32, name="w1_raw0")
         nc.sync.dma_start(w1_raw[:], w1.rearrange("(p j) c -> p j c", j=PACK))
@@ -95,8 +98,8 @@ def tile_picked_phpq_gelu_po_kernel(
             nc.sync.dma_start(
                 xs_plane[32 * q : 32 * q + 4, :].bitcast(I32), xs_got[32 * q : 32 * q + 32 : 8, :].bitcast(I32)
             )
-        for a, b in POS_PIECES:
-            nc.sync.dma_start(pos_sb[:, :, a:b], pos_rows[:, :, a:b])
+        for a in range(0, S, POS_PIECE):
+            nc.sync.dma_start(pos_sb[:, :, a : a + POS_PIECE], pos_rows[:, :, a : a + POS_PIECE])
 
         xq_early = keep.tile([P, EARLY], U32, name="xq_early", align_bytes=64)
         nc.vector.tensor_copy(xq_early[:], xw_win[:].indirect(offsets[:, 0 : EARLY // 16]))
@@ -124,6 +127,7 @@ def tile_picked_phpq_gelu_po_kernel(
 
         xq_late = shared.tile([P, S - EARLY], U32, name="xq_late", align_bytes=64, offset=XQ_LATE_AT)
         nc.vector.tensor_copy(xq_late[:], xw_win[:].indirect(offsets[:, EARLY // 16 : S // 16]))
+
         w2_q = shared.tile([P, H], I32, name="w2_q", align_bytes=64, offset=W1_BF_AT)
         nc.gpsimd.tensor_copy(
             w2_q[:].rearrange("p (t b i) -> p b t i", t=PACK, i=4),
@@ -153,7 +157,7 @@ def tile_picked_phpq_gelu_po_kernel(
                 )
             return bank
 
-        pres = {}
+        pre = {}
         h_bf = {}
         acc2 = {}
         y = {}
@@ -168,16 +172,15 @@ def tile_picked_phpq_gelu_po_kernel(
             early = EARLY // UNIT
             codes = xq_early[:, cols] if u < early else xq_late[:, columns(u - early, u - early + 1)]
             bank = product("acc1", w1_q, w1_s, codes, xs_plane[:, cols])
-            pre = keep.tile([P, PACK, UNIT], F32, name=f"pre{u}")
-            nc.vector.tensor_tensor(pre[:], bank[:], pos_sb[:, :, cols], ADD)
-            pres[u] = pre
+            pre[u] = keep.tile([P, PACK, UNIT], F32, name=f"pre{u}")
+            nc.vector.tensor_tensor(pre[u][:], bank[:], pos_sb[:, :, cols], ADD)
 
         def gelu(u):
-            pre = pres[u]
-            h_bf[u] = shared.tile([P, UNIT, PACK], BF16, name=f"h_bf{u}", align_bytes=64, offset=H_BF_AT + u * 1024)
+            at = H_BF_AT + u * UNIT_BF_BYTES
+            h_bf[u] = shared.tile([P, UNIT, PACK], BF16, name=f"h_bf{u}", align_bytes=64, offset=at)
             nc.scalar.activation(
                 h_bf[u][:].rearrange("p (g i) t -> p g t i", i=2),
-                pre[:].rearrange("p t (g i) -> p g t i", i=2),
+                pre[u][:].rearrange("p t (g i) -> p g t i", i=2),
                 GELU,
             )
 
@@ -191,7 +194,7 @@ def tile_picked_phpq_gelu_po_kernel(
 
         def leave(u):
             tile, first = y[u]
-            copy = nc.vector.tensor_copy if u == VECTOR_COPY_UNIT else nc.scalar.copy
+            copy = nc.vector.tensor_copy if u in VECTOR_COPY_UNITS else nc.scalar.copy
             copy(tile[:, :, columns(u - first, u - first + 1)], acc2[u][:])
             if (first, u + 1) in OUT_GROUPS:
                 nc.sync.dma_start(out_rows[:, :, columns(first, u + 1)], tile[:])
@@ -200,7 +203,7 @@ def tile_picked_phpq_gelu_po_kernel(
             tile, first = y[u]
             src = tile[:, :, columns(u - first, u - first + 1)].rearrange("p t (g i) -> p g t i", i=2)
             if u in GPSIMD_BEHIND:
-                at = H_BF_AT + GPSIMD_BEHIND[u] * 1024
+                at = H_BF_AT + GPSIMD_BEHIND[u] * UNIT_BF_BYTES
                 y_bf[u] = shared.tile([P, UNIT, PACK], BF16, name=f"y_bf{u}", align_bytes=64, offset=at)
                 nc.gpsimd.tensor_scalar(y_bf[u][:].rearrange("p (g i) t -> p g t i", i=2), src, 1.0, 0.0, MULT, ADD)
             else:
@@ -213,9 +216,9 @@ def tile_picked_phpq_gelu_po_kernel(
                 scales=out_s[4 * (u // 2) : P, columns(u % 2, u % 2 + 1)],
                 in_=y_bf[u][:].rearrange("p n t -> p (n t)"),
             )
-            if u % 2 == 1:
-                pair = columns(u - 1, u + 1)
-                nc.sync.dma_start(out_words[:, pair], out_q[:, pair].bitcast(I32))
+            for a, b in WORD_GROUPS:
+                if u == b - 1:
+                    nc.sync.dma_start(out_words[:, columns(a, b)], out_q[:, columns(a, b)].bitcast(I32))
 
         for u in range(3):
             layer1(u)
@@ -224,6 +227,7 @@ def tile_picked_phpq_gelu_po_kernel(
         leave(0)
         layer1(3)
         gelu(3)
+
         layer2(1)
         layer2(2)
         layer1(4)
@@ -232,6 +236,7 @@ def tile_picked_phpq_gelu_po_kernel(
         layer1(5)
         leave(2)
         gelu(5)
+
         layer2(3)
         layer2(4)
         leave(3)
@@ -240,7 +245,8 @@ def tile_picked_phpq_gelu_po_kernel(
         gelu(6)
         leave(4)
         gelu(7)
-        for u in range(5, 8):
+
+        for u in range(5, N_UNITS):
             layer2(u)
             leave(u)
 

@@ -23,15 +23,14 @@ UNIT = 128
 N_UNITS = S // UNIT
 BANKS = 4
 
-X_FIRST = T // 4
-XS_VECTOR = 3 * T // 4
+X_FIRST = T // 8
 EARLY = 768
 W1_SCALAR_GROUPS = 104
 POS_PIECE = 2 * UNIT
 VECTOR_COPY_UNITS = (1, 4)
 GPSIMD_BEHIND = {0: 2, 1: 4}
 OUT_GROUPS = ((0, 1), (1, 3), (3, 4), (4, 5), (5, 6), (6, 8))
-WORD_GROUPS = ((0, 3), (3, 6), (6, 8))
+WORD_GROUPS = ((0, 2), (2, 6), (6, 8))
 
 POS_BYTES = PACK * S * 4
 XS_WIN_AT = POS_BYTES - 512
@@ -58,8 +57,7 @@ def tile_picked_phpq_gelu_po_kernel(
 
         xs_win = shared.tile([P, T], U8, name="xs_win", offset=XS_WIN_AT)
         w2s_raw = keep.tile([P, H], U8, name="w2s_raw")
-        nc.vector.memset(xs_win[:, 0:XS_VECTOR].bitcast(I32), 0)
-        nc.gpsimd.memset(xs_win[:, XS_VECTOR:T].bitcast(I32), 0)
+        nc.vector.memset(xs_win[:].bitcast(I32), 0)
         nc.vector.memset(w2s_raw[:].bitcast(I32), 0)
 
         for q in range(QUADRANTS):
@@ -167,22 +165,27 @@ def tile_picked_phpq_gelu_po_kernel(
             for u in range(a, b):
                 y[u] = (tile, a)
 
+        def parts(u):
+            return ((0, UNIT // 2), (UNIT // 2, UNIT)) if u == 0 else ((0, UNIT),)
+
         def layer1(u):
             cols = columns(u, u + 1)
             early = EARLY // UNIT
             codes = xq_early[:, cols] if u < early else xq_late[:, columns(u - early, u - early + 1)]
             bank = product("acc1", w1_q, w1_s, codes, xs_plane[:, cols])
             pre[u] = keep.tile([P, PACK, UNIT], F32, name=f"pre{u}")
-            nc.vector.tensor_tensor(pre[u][:], bank[:], pos_sb[:, :, cols], ADD)
+            for a, b in parts(u):
+                nc.vector.tensor_tensor(pre[u][:, :, a:b], bank[:, :, a:b], pos_sb[:, :, cols][:, :, a:b], ADD)
 
         def gelu(u):
             at = H_BF_AT + u * UNIT_BF_BYTES
             h_bf[u] = shared.tile([P, UNIT, PACK], BF16, name=f"h_bf{u}", align_bytes=64, offset=at)
-            nc.scalar.activation(
-                h_bf[u][:].rearrange("p (g i) t -> p g t i", i=2),
-                pre[u][:].rearrange("p t (g i) -> p g t i", i=2),
-                GELU,
-            )
+            for a, b in parts(u):
+                nc.scalar.activation(
+                    h_bf[u][:, a:b, :].rearrange("p (g i) t -> p g t i", i=2),
+                    pre[u][:, :, a:b].rearrange("p t (g i) -> p g t i", i=2),
+                    GELU,
+                )
 
         def layer2(u):
             h_q = keep.tile([P, UNIT], U32, name=f"h_q{u}", align_bytes=64)

@@ -211,7 +211,8 @@ def tile_picked_phpq_gelu_po_kernel(
                 nc.gpsimd.tensor_scalar(y_bf[u][:].rearrange("p (g i) t -> p g t i", i=2), src, 1.0, 0.0, MULT, ADD)
             else:
                 y_bf[u] = keep.tile([P, UNIT, PACK], BF16, name=f"y_bf{u}", align_bytes=64)
-                nc.vector.tensor_copy(y_bf[u][:].rearrange("p (g i) t -> p g t i", i=2), src)
+                copy = nc.scalar.copy if u == N_UNITS - 1 else nc.vector.tensor_copy
+                copy(y_bf[u][:].rearrange("p (g i) t -> p g t i", i=2), src)
 
         def quantize_y(u):
             nc.vector.quantize_mx(

@@ -102,11 +102,14 @@ def tile_picked_phpq_gelu_po_kernel(
         xq_early = keep.tile([P, EARLY], U32, name="xq_early", align_bytes=64)
         nc.vector.tensor_copy(xq_early[:], xw_win[:].indirect(offsets[:, 0 : EARLY // 16]))
 
-        w1_bf = shared.tile([P, PACK, P, PACK], BF16, name="w1_bf", align_bytes=64, offset=W1_BF_AT)
+        w1_bf = [
+            shared.tile([P, 2, P, PACK], BF16, name=f"w1_bf{s}", align_bytes=64, offset=W1_BF_AT + (1 - s) * H * PACK)
+            for s in range(2)
+        ]
 
         def round_w1(copy, s, m0, m1):
             copy(
-                w1_bf[:, 2 * s : 2 * s + 2, m0:m1, :].rearrange("p e m j -> p m j e"),
+                w1_bf[s][:, :, m0:m1, :].rearrange("p e m j -> p m j e"),
                 w1_raw[:].rearrange("p j (m t) -> p m j t", t=PACK)[:, m0:m1, :, 2 * s : 2 * s + 2],
             )
 
@@ -120,7 +123,7 @@ def tile_picked_phpq_gelu_po_kernel(
             nc.vector.quantize_mx(
                 out=w1_q[:, cols].bitcast(FP8X4),
                 scales=w1_s[:, cols],
-                in_=w1_bf[:, t, :, :].rearrange("p m j -> p (m j)"),
+                in_=w1_bf[t // 2][:, t % 2, :, :].rearrange("p m j -> p (m j)"),
             )
 
         xq_late = shared.tile([P, S - EARLY], U32, name="xq_late", align_bytes=64, offset=XQ_LATE_AT)
@@ -182,8 +185,8 @@ def tile_picked_phpq_gelu_po_kernel(
             h_bf[u] = shared.tile([P, UNIT, PACK], BF16, name=f"h_bf{u}", align_bytes=64, offset=at)
             for a, b in parts(u):
                 nc.scalar.activation(
-                    h_bf[u][:, a:b, :].rearrange("p (g i) t -> p g t i", i=2),
-                    pre[u][:, :, a:b].rearrange("p t (g i) -> p g t i", i=2),
+                    h_bf[u][:, a:b, :].rearrange("p (g i) t -> p g t i", i=4),
+                    pre[u][:, :, a:b].rearrange("p t (g i) -> p g t i", i=4),
                     GELU,
                 )
 
@@ -204,15 +207,15 @@ def tile_picked_phpq_gelu_po_kernel(
 
         def round_y(u):
             tile, first = y[u]
-            src = tile[:, :, columns(u - first, u - first + 1)].rearrange("p t (g i) -> p g t i", i=2)
+            src = tile[:, :, columns(u - first, u - first + 1)].rearrange("p t (g i) -> p g t i", i=4)
             if u in GPSIMD_BEHIND:
                 at = H_BF_AT + GPSIMD_BEHIND[u] * UNIT_BF_BYTES
                 y_bf[u] = shared.tile([P, UNIT, PACK], BF16, name=f"y_bf{u}", align_bytes=64, offset=at)
-                nc.gpsimd.tensor_scalar(y_bf[u][:].rearrange("p (g i) t -> p g t i", i=2), src, 1.0, 0.0, MULT, ADD)
+                nc.gpsimd.tensor_scalar(y_bf[u][:].rearrange("p (g i) t -> p g t i", i=4), src, 1.0, 0.0, MULT, ADD)
             else:
                 y_bf[u] = keep.tile([P, UNIT, PACK], BF16, name=f"y_bf{u}", align_bytes=64)
                 copy = nc.scalar.copy if u == N_UNITS - 1 else nc.vector.tensor_copy
-                copy(y_bf[u][:].rearrange("p (g i) t -> p g t i", i=2), src)
+                copy(y_bf[u][:].rearrange("p (g i) t -> p g t i", i=4), src)
 
         def quantize_y(u):
             nc.vector.quantize_mx(

@@ -21,6 +21,7 @@ PACK = 4
 QUADRANTS = 4
 UNIT = 128
 N_UNITS = S // UNIT
+DMA_ALIGN = 256
 BANKS = 4
 
 X_FIRST = T // 8
@@ -49,14 +50,14 @@ def tile_picked_phpq_gelu_po_kernel(
         shared = ctx.enter_context(tc.tile_pool(name="shared", bufs=1))
         psum = ctx.enter_context(tc.psum_pool(name="psum", bufs=BANKS))
 
-        xw_win = keep.tile([P, T], U32, name="xw_win")
+        xw_win = keep.tile([P, T], U32, name="xw_win", align_bytes=DMA_ALIGN)
         x_rows = x_words[0].rearrange("p n t -> p (n t)").bitcast(I32)
         nc.sync.dma_start(xw_win[:, 0:X_FIRST].bitcast(I32), x_rows[:, 0:X_FIRST])
-        offsets = keep.tile([P, S // 16], U16, name="offsets")
+        offsets = keep.tile([P, S // 16], U16, name="offsets", align_bytes=DMA_ALIGN)
         nc.sync.dma_start(offsets[:], offs)
 
-        xs_win = shared.tile([P, T], U8, name="xs_win", offset=XS_WIN_AT)
-        w2s_raw = keep.tile([P, H], U8, name="w2s_raw")
+        xs_win = shared.tile([P, T], U8, name="xs_win", align_bytes=DMA_ALIGN, offset=XS_WIN_AT)
+        w2s_raw = keep.tile([P, H], U8, name="w2s_raw", align_bytes=DMA_ALIGN)
         nc.vector.memset(xs_win[:].bitcast(I32), 0)
         nc.vector.memset(w2s_raw[:].bitcast(I32), 0)
 
@@ -73,24 +74,24 @@ def tile_picked_phpq_gelu_po_kernel(
 
         nc.sync.dma_start(xw_win[:, X_FIRST:T].bitcast(I32), x_rows[:, X_FIRST:T])
 
-        w1_raw = keep.tile([P, PACK, H], F32, name="w1_raw0")
+        w1_raw = keep.tile([P, PACK, H], F32, name="w1_raw", align_bytes=DMA_ALIGN)
         nc.sync.dma_start(w1_raw[:], w1.rearrange("(p j) c -> p j c", j=PACK))
 
         pos_rows = pos.rearrange("(p t) s -> p t s", t=PACK)
-        w2w_raw = keep.tile([P, H], I32, name="w2w_raw")
+        w2w_raw = keep.tile([P, H], I32, name="w2w_raw", align_bytes=DMA_ALIGN)
         nc.sync.dma_start(w2w_raw[:], w2_words[0].rearrange("p n t -> p (n t)").bitcast(I32))
 
-        xs_plane = keep.tile([P, S], U8, name="xs_plane", align_bytes=64)
+        xs_plane = keep.tile([P, S], U8, name="xs_plane", align_bytes=DMA_ALIGN)
         nc.vector.memset(xs_plane[:].bitcast(I32), 0)
 
-        pos_sb = shared.tile([P, PACK, S], F32, name="pos_sb", offset=0)
+        pos_sb = shared.tile([P, PACK, S], F32, name="pos_sb", align_bytes=DMA_ALIGN, offset=0)
 
         w2_s = keep.tile([P, H], U8, name="w2_s", align_bytes=64)
         nc.gpsimd.tensor_copy(
             w2_s[:].rearrange("p (t m) -> p t m", t=PACK), w2s_raw[:].rearrange("p (m t) -> p t m", t=PACK)
         )
 
-        xs_got = keep.tile([P, S], U8, name="xs_got")
+        xs_got = keep.tile([P, S], U8, name="xs_got", align_bytes=DMA_ALIGN)
         nc.vector.tensor_copy(xs_got[:], xs_win[:].indirect(offsets[:]))
         for q in range(QUADRANTS):
             nc.sync.dma_start(
@@ -135,8 +136,8 @@ def tile_picked_phpq_gelu_po_kernel(
             w2w_raw[:].rearrange("p (b i t) -> p b t i", t=PACK, i=4),
         )
 
-        out_q = keep.tile([P, S], U32, name="out_q", align_bytes=64)
-        out_s = keep.tile([P, 2 * UNIT], U8, name="out_s", align_bytes=64)
+        out_q = keep.tile([P, S], U32, name="out_q", align_bytes=DMA_ALIGN)
+        out_s = keep.tile([P, 2 * UNIT], U8, name="out_s", align_bytes=DMA_ALIGN)
         out_rows = out_0.rearrange("(p t) s -> p t s", t=PACK)
         out_words = out_1[0].rearrange("p n t -> p (n t)").bitcast(I32)
 
@@ -164,7 +165,7 @@ def tile_picked_phpq_gelu_po_kernel(
         y = {}
         y_bf = {}
         for a, b in OUT_GROUPS:
-            tile = keep.tile([P, PACK, (b - a) * UNIT], F32, name=f"y{a}")
+            tile = keep.tile([P, PACK, (b - a) * UNIT], F32, name=f"y{a}", align_bytes=DMA_ALIGN)
             for u in range(a, b):
                 y[u] = (tile, a)
 

@@ -19,6 +19,7 @@ MULT = mybir.AluOpType.mult
 P = 128
 PACK = 4
 QUADRANTS = 4
+ROWS = 4
 UNIT = 128
 N_UNITS = S // UNIT
 DMA_ALIGN = 256
@@ -61,11 +62,9 @@ def tile_picked_phpq_gelu_po_kernel(
         nc.vector.memset(xs_win[:].bitcast(I32), 0)
         nc.vector.memset(w2s_raw[:].bitcast(I32), 0)
 
-        for q in range(QUADRANTS):
-            nc.scalar.dma_start(
-                w2s_raw[32 * q : 32 * q + 4, :].bitcast(I32), w2_scales[0, 4 * q : 4 * q + 4, :].bitcast(I32)
-            )
-        nc.sync.dma_start(xs_win[0:P:8, :].bitcast(I32), x_scales[0].bitcast(I32))
+        for c in range(ROWS):
+            nc.scalar.dma_start(w2s_raw[c:P:32, :].bitcast(I32), w2_scales[0, c:16:ROWS, :].bitcast(I32))
+        nc.sync.dma_start(xs_win[4:P:8, :].bitcast(I32), x_scales[0].bitcast(I32))
 
         warm = keep.tile([P, 1], F32, name="warm")
         nc.vector.memset(warm[:], 0.0)
@@ -93,10 +92,8 @@ def tile_picked_phpq_gelu_po_kernel(
 
         xs_got = keep.tile([P, S], U8, name="xs_got", align_bytes=DMA_ALIGN)
         nc.vector.tensor_copy(xs_got[:], xs_win[:].indirect(offsets[:]))
-        for q in range(QUADRANTS):
-            nc.sync.dma_start(
-                xs_plane[32 * q : 32 * q + 4, :].bitcast(I32), xs_got[32 * q : 32 * q + 32 : 8, :].bitcast(I32)
-            )
+        for c in range(ROWS):
+            nc.sync.dma_start(xs_plane[c:P:32, :].bitcast(I32), xs_got[8 * c + 4 : P : 32, :].bitcast(I32))
         for a in range(0, S, POS_PIECE):
             nc.sync.dma_start(pos_sb[:, :, a : a + POS_PIECE], pos_rows[:, :, a : a + POS_PIECE])
 

@@ -30,7 +30,7 @@ EARLY = 768
 W1_SCALAR_GROUPS = 104
 POS_PIECE = 2 * UNIT
 VECTOR_COPY_UNITS = (1, 4)
-GPSIMD_BEHIND = {0: 2, 1: 4}
+GPSIMD_BEHIND = {0: 2, 1: 3}
 OUT_GROUPS = ((0, 1), (1, 3), (3, 4), (4, 5), (5, 6), (6, 8))
 WORD_GROUPS = ((0, 2), (2, 6), (6, 8))
 
@@ -205,15 +205,17 @@ def tile_picked_phpq_gelu_po_kernel(
 
         def round_y(u):
             tile, first = y[u]
-            src = tile[:, :, columns(u - first, u - first + 1)].rearrange("p t (g i) -> p g t i", i=4)
+            unit = tile[:, :, columns(u - first, u - first + 1)]
             if u in GPSIMD_BEHIND:
                 at = H_BF_AT + GPSIMD_BEHIND[u] * UNIT_BF_BYTES
                 y_bf[u] = shared.tile([P, UNIT, PACK], BF16, name=f"y_bf{u}", align_bytes=64, offset=at)
-                nc.gpsimd.tensor_scalar(y_bf[u][:].rearrange("p (g i) t -> p g t i", i=4), src, 1.0, 0.0, MULT, ADD)
+                nc.gpsimd.tensor_scalar(y_bf[u][:], unit.rearrange("p t n -> p n t"), 1.0, 0.0, MULT, ADD)
             else:
                 y_bf[u] = keep.tile([P, UNIT, PACK], BF16, name=f"y_bf{u}", align_bytes=64)
                 copy = nc.scalar.copy if u == N_UNITS - 1 else nc.vector.tensor_copy
-                copy(y_bf[u][:].rearrange("p (g i) t -> p g t i", i=4), src)
+                copy(
+                    y_bf[u][:].rearrange("p (g i) t -> p g t i", i=4), unit.rearrange("p t (g i) -> p g t i", i=4)
+                )
 
         def quantize_y(u):
             nc.vector.quantize_mx(
@@ -248,10 +250,12 @@ def tile_picked_phpq_gelu_po_kernel(
         layer1(6)
         layer1(7)
         gelu(6)
+        layer2(5)
         leave(4)
         gelu(7)
+        leave(5)
 
-        for u in range(5, N_UNITS):
+        for u in range(6, N_UNITS):
             layer2(u)
             leave(u)
 

@@ -212,10 +212,11 @@ def tile_picked_phpq_gelu_po_kernel(
                 nc.gpsimd.tensor_scalar(y_bf[u][:], unit.rearrange("p t n -> p n t"), 1.0, 0.0, MULT, ADD)
             else:
                 y_bf[u] = keep.tile([P, UNIT, PACK], BF16, name=f"y_bf{u}", align_bytes=64)
-                copy = nc.scalar.copy if u == N_UNITS - 1 else nc.vector.tensor_copy
-                copy(
-                    y_bf[u][:].rearrange("p (g i) t -> p g t i", i=4), unit.rearrange("p t (g i) -> p g t i", i=4)
-                )
+                dst = y_bf[u][:].rearrange("p (g i) t -> p g t i", i=4)
+                if u == N_UNITS - 1:
+                    nc.scalar.copy(dst, acc2[u][:].rearrange("p t (g i) -> p g t i", i=4))
+                else:
+                    nc.vector.tensor_copy(dst, unit.rearrange("p t (g i) -> p g t i", i=4))
 
         def quantize_y(u):
             nc.vector.quantize_mx(

@@ -199,9 +199,12 @@ def tile_picked_phpq_gelu_po_kernel(
         def leave(u):
             tile, first = y[u]
             copy = nc.vector.tensor_copy if u in VECTOR_COPY_UNITS else nc.scalar.copy
-            copy(tile[:, :, columns(u - first, u - first + 1)], acc2[u][:])
-            if (first, u + 1) in OUT_GROUPS:
-                nc.sync.dma_start(out_rows[:, :, columns(first, u + 1)], tile[:])
+            step = PACK // 2 if u == N_UNITS - 1 else PACK
+            for t in range(0, PACK, step):
+                tiles = slice(t, t + step)
+                copy(tile[:, tiles, columns(u - first, u - first + 1)], acc2[u][:, tiles, :])
+                if (first, u + 1) in OUT_GROUPS:
+                    nc.sync.dma_start(out_rows[:, tiles, columns(first, u + 1)], tile[:, tiles, :])
 
         def round_y(u):
             tile, first = y[u]

from contextlib import ExitStack

import concourse.mybir as mybir

K, T, S, H = 512, 2048, 1024, 512
FLOPS = 2 * K * H * S + 2 * H * H * S

F32 = mybir.dt.float32
BF16 = mybir.dt.bfloat16
I32 = mybir.dt.int32
U32 = mybir.dt.uint32
U16 = mybir.dt.uint16
U8 = mybir.dt.uint8
FP8X4 = mybir.dt.float8_e4m3fn_x4
GELU = mybir.ActivationFunctionType.Gelu_apprx_tanh
ADD = mybir.AluOpType.add
MULT = mybir.AluOpType.mult

P = 128
PACK = 4
QUADRANTS = 4
ROWS = 4
UNIT = 128
N_UNITS = S // UNIT
DMA_ALIGN = 256
BANKS = 4

X_FIRST = T // 8
EARLY = 768
W1_SCALAR_GROUPS = 104
POS_PIECE = 2 * UNIT
VECTOR_COPY_UNITS = (1, 4)
GPSIMD_BEHIND = {0: 2, 1: 3}
OUT_GROUPS = ((0, 1), (1, 3), (3, 4), (4, 5), (5, 6), (6, 8))
WORD_GROUPS = ((0, 2), (2, 6), (6, 8))

POS_BYTES = PACK * S * 4
XS_WIN_AT = POS_BYTES - 512
W1_BF_AT = POS_BYTES + T
XQ_LATE_AT = W1_BF_AT + 2560
H_BF_AT = W1_BF_AT + PACK * H * 2
UNIT_BF_BYTES = PACK * UNIT * 2


def tile_picked_phpq_gelu_po_kernel(
    tc, x_words, x_scales, w1, w2_words, w2_scales, pos, offs, out_0, out_1, out_2
):
    nc = tc.nc
    with ExitStack() as ctx:
        keep = ctx.enter_context(tc.tile_pool(name="keep", bufs=1))
        shared = ctx.enter_context(tc.tile_pool(name="shared", bufs=1))
        psum = ctx.enter_context(tc.psum_pool(name="psum", bufs=BANKS))

        xw_win = keep.tile([P, T], U32, name="xw_win", align_bytes=DMA_ALIGN)
        x_rows = x_words[0].rearrange("p n t -> p (n t)").bitcast(I32)
        nc.sync.dma_start(xw_win[:, 0:X_FIRST].bitcast(I32), x_rows[:, 0:X_FIRST])
        offsets = keep.tile([P, S // 16], U16, name="offsets", align_bytes=DMA_ALIGN)
        nc.sync.dma_start(offsets[:], offs)

        xs_win = shared.tile([P, T], U8, name="xs_win", align_bytes=DMA_ALIGN, offset=XS_WIN_AT)
        w2s_raw = keep.tile([P, H], U8, name="w2s_raw", align_bytes=DMA_ALIGN)
        nc.vector.memset(xs_win[:].bitcast(I32), 0)
        nc.vector.memset(w2s_raw[:].bitcast(I32), 0)

        for c in range(ROWS):
            nc.scalar.dma_start(w2s_raw[c:P:32, :].bitcast(I32), w2_scales[0, c:16:ROWS, :].bitcast(I32))
        nc.sync.dma_start(xs_win[4:P:8, :].bitcast(I32), x_scales[0].bitcast(I32))

        warm = keep.tile([P, 1], F32, name="warm")
        nc.vector.memset(warm[:], 0.0)
        warm_out = keep.tile([P, 1], F32, name="warm_out")
        nc.scalar.activation(warm_out[:], warm[:], GELU)

        nc.sync.dma_start(xw_win[:, X_FIRST:T].bitcast(I32), x_rows[:, X_FIRST:T])

        w1_raw = keep.tile([P, PACK, H], F32, name="w1_raw", align_bytes=DMA_ALIGN)
        nc.sync.dma_start(w1_raw[:], w1.rearrange("(p j) c -> p j c", j=PACK))

        pos_rows = pos.rearrange("(p t) s -> p t s", t=PACK)
        w2w_raw = keep.tile([P, H], I32, name="w2w_raw", align_bytes=DMA_ALIGN)
        nc.sync.dma_start(w2w_raw[:], w2_words[0].rearrange("p n t -> p (n t)").bitcast(I32))

        xs_plane = keep.tile([P, S], U8, name="xs_plane", align_bytes=DMA_ALIGN)
        nc.vector.memset(xs_plane[:].bitcast(I32), 0)

        pos_sb = shared.tile([P, PACK, S], F32, name="pos_sb", align_bytes=DMA_ALIGN, offset=0)

        w2_s = keep.tile([P, H], U8, name="w2_s", align_bytes=64)
        nc.gpsimd.tensor_copy(
            w2_s[:].rearrange("p (t m) -> p t m", t=PACK), w2s_raw[:].rearrange("p (m t) -> p t m", t=PACK)
        )

        xs_got = keep.tile([P, S], U8, name="xs_got", align_bytes=DMA_ALIGN)
        nc.vector.tensor_copy(xs_got[:], xs_win[:].indirect(offsets[:]))
        for c in range(ROWS):
            nc.sync.dma_start(xs_plane[c:P:32, :].bitcast(I32), xs_got[8 * c + 4 : P : 32, :].bitcast(I32))
        for a in range(0, S, POS_PIECE):
            nc.sync.dma_start(pos_sb[:, :, a : a + POS_PIECE], pos_rows[:, :, a : a + POS_PIECE])

        xq_early = keep.tile([P, EARLY], U32, name="xq_early", align_bytes=64)
        nc.vector.tensor_copy(xq_early[:], xw_win[:].indirect(offsets[:, 0 : EARLY // 16]))

        w1_bf = [
            shared.tile([P, 2, P, PACK], BF16, name=f"w1_bf{s}", align_bytes=64, offset=W1_BF_AT + (1 - s) * H * PACK)
            for s in range(2)
        ]

        def round_w1(copy, s, m0, m1):
            copy(
                w1_bf[s][:, :, m0:m1, :].rearrange("p e m j -> p m j e"),
                w1_raw[:].rearrange("p j (m t) -> p m j t", t=PACK)[:, m0:m1, :, 2 * s : 2 * s + 2],
            )

        round_w1(nc.vector.tensor_copy, 0, 0, P)
        round_w1(nc.scalar.copy, 1, 0, W1_SCALAR_GROUPS)
        round_w1(nc.vector.tensor_copy, 1, W1_SCALAR_GROUPS, P)
        w1_q = keep.tile([P, H], U32, name="w1_q", align_bytes=64)
        w1_s = keep.tile([P, H], U8, name="w1_s", align_bytes=64)
        for t in range(PACK):
            cols = slice(t * P, (t + 1) * P)
            nc.vector.quantize_mx(
                out=w1_q[:, cols].bitcast(FP8X4),
                scales=w1_s[:, cols],
                in_=w1_bf[t // 2][:, t % 2, :, :].rearrange("p m j -> p (m j)"),
            )

        xq_late = shared.tile([P, S - EARLY], U32, name="xq_late", align_bytes=64, offset=XQ_LATE_AT)
        nc.vector.tensor_copy(xq_late[:], xw_win[:].indirect(offsets[:, EARLY // 16 : S // 16]))

        w2_q = shared.tile([P, H], I32, name="w2_q", align_bytes=64, offset=W1_BF_AT)
        nc.gpsimd.tensor_copy(
            w2_q[:].rearrange("p (t b i) -> p b t i", t=PACK, i=4),
            w2w_raw[:].rearrange("p (b i t) -> p b t i", t=PACK, i=4),
        )

        out_q = keep.tile([P, S], U32, name="out_q", align_bytes=DMA_ALIGN)
        out_s = keep.tile([P, 2 * UNIT], U8, name="out_s", align_bytes=DMA_ALIGN)
        out_rows = out_0.rearrange("(p t) s -> p t s", t=PACK)
        out_words = out_1[0].rearrange("p n t -> p (n t)").bitcast(I32)

        def columns(u0, u1):
            return slice(u0 * UNIT, u1 * UNIT)

        def product(name, w_q, w_s, codes, scales):
            bank = psum.tile([P, PACK, UNIT], F32, name=name)
            for t in range(PACK):
                cols = slice(t * P, (t + 1) * P)
                nc.tensor.matmul_mx(
                    out=bank[:, t, :],
                    lhsT=w_q[:, cols].bitcast(FP8X4),
                    lhsT_scale=w_s[:, cols],
                    rhs=codes.bitcast(FP8X4),
                    rhs_scale=scales,
                    start=True,
                    stop=True,
                )
            return bank

        pre = {}
        h_bf = {}
        acc2 = {}
        y = {}
        y_bf = {}
        for a, b in OUT_GROUPS:
            tile = keep.tile([P, PACK, (b - a) * UNIT], F32, name=f"y{a}", align_bytes=DMA_ALIGN)
            for u in range(a, b):
                y[u] = (tile, a)

        def parts(u):
            return ((0, UNIT // 2), (UNIT // 2, UNIT)) if u == 0 else ((0, UNIT),)

        def layer1(u):
            cols = columns(u, u + 1)
            early = EARLY // UNIT
            codes = xq_early[:, cols] if u < early else xq_late[:, columns(u - early, u - early + 1)]
            bank = product("acc1", w1_q, w1_s, codes, xs_plane[:, cols])
            pre[u] = keep.tile([P, PACK, UNIT], F32, name=f"pre{u}")
            for a, b in parts(u):
                nc.vector.tensor_tensor(pre[u][:, :, a:b], bank[:, :, a:b], pos_sb[:, :, cols][:, :, a:b], ADD)

        def gelu(u):
            at = H_BF_AT + u * UNIT_BF_BYTES
            h_bf[u] = shared.tile([P, UNIT, PACK], BF16, name=f"h_bf{u}", align_bytes=64, offset=at)
            for a, b in parts(u):
                nc.scalar.activation(
                    h_bf[u][:, a:b, :].rearrange("p (g i) t -> p g t i", i=4),
                    pre[u][:, :, a:b].rearrange("p t (g i) -> p g t i", i=4),
                    GELU,
                )

        def layer2(u):
            h_q = keep.tile([P, UNIT], U32, name=f"h_q{u}", align_bytes=64)
            h_s = keep.tile([P, UNIT], U8, name=f"h_s{u}", align_bytes=64)
            nc.vector.quantize_mx(
                out=h_q[:].bitcast(FP8X4), scales=h_s[:], in_=h_bf[u][:].rearrange("p n t -> p (n t)")
            )
            acc2[u] = product("acc2", w2_q, w2_s, h_q[:], h_s[:])

        def leave(u):
            tile, first = y[u]
            copy = nc.vector.tensor_copy if u in VECTOR_COPY_UNITS else nc.scalar.copy
            step = PACK // 2 if u == N_UNITS - 1 else PACK
            for t in range(0, PACK, step):
                tiles = slice(t, t + step)
                copy(tile[:, tiles, columns(u - first, u - first + 1)], acc2[u][:, tiles, :])
                if (first, u + 1) in OUT_GROUPS:
                    nc.sync.dma_start(out_rows[:, tiles, columns(first, u + 1)], tile[:, tiles, :])

        def round_y(u):
            tile, first = y[u]
            unit = tile[:, :, columns(u - first, u - first + 1)]
            if u in GPSIMD_BEHIND:
                at = H_BF_AT + GPSIMD_BEHIND[u] * UNIT_BF_BYTES
                y_bf[u] = shared.tile([P, UNIT, PACK], BF16, name=f"y_bf{u}", align_bytes=64, offset=at)
                nc.gpsimd.tensor_scalar(y_bf[u][:], unit.rearrange("p t n -> p n t"), 1.0, 0.0, MULT, ADD)
            else:
                y_bf[u] = keep.tile([P, UNIT, PACK], BF16, name=f"y_bf{u}", align_bytes=64)
                dst = y_bf[u][:].rearrange("p (g i) t -> p g t i", i=4)
                if u == N_UNITS - 1:
                    nc.scalar.copy(dst, acc2[u][:].rearrange("p t (g i) -> p g t i", i=4))
                else:
                    nc.vector.tensor_copy(dst, unit.rearrange("p t (g i) -> p g t i", i=4))

        def quantize_y(u):
            nc.vector.quantize_mx(
                out=out_q[:, columns(u, u + 1)].bitcast(FP8X4),
                scales=out_s[4 * (u // 2) : P, columns(u % 2, u % 2 + 1)],
                in_=y_bf[u][:].rearrange("p n t -> p (n t)"),
            )
            for a, b in WORD_GROUPS:
                if u == b - 1:
                    nc.sync.dma_start(out_words[:, columns(a, b)], out_q[:, columns(a, b)].bitcast(I32))

        for u in range(3):
            layer1(u)
            gelu(u)
        layer2(0)
        leave(0)
        layer1(3)
        gelu(3)

        layer2(1)
        layer2(2)
        layer1(4)
        gelu(4)
        leave(1)
        layer1(5)
        leave(2)
        gelu(5)

        layer2(3)
        layer2(4)
        leave(3)
        layer1(6)
        layer1(7)
        gelu(6)
        layer2(5)
        leave(4)
        gelu(7)
        leave(5)

        for u in range(6, N_UNITS):
            layer2(u)
            leave(u)

        for u in range(N_UNITS + 1):
            if u < N_UNITS:
                round_y(u)
            if u >= 1:
                quantize_y(u - 1)

        for q in range(QUADRANTS):
            eng = nc.sync if q % 2 == 0 else nc.scalar
            eng.dma_start(
                out_2[0, 4 * q : 4 * q + 4, :].bitcast(I32).rearrange("c (g n) -> g c n", g=N_UNITS // 2),
                out_s[32 * q : 32 * q + 16, :].bitcast(I32),
            )
